import numpy as np
import ml_dtypes


def mxq(x, axis, fmt="e4m3"):
    dtype, down = {"e4m3": (ml_dtypes.float8_e4m3fn, 7), "e5m2": (ml_dtypes.float8_e5m2, 14)}[fmt]
    v = np.moveaxis(np.asarray(x, np.float32).astype(ml_dtypes.bfloat16).astype(np.float64), axis, -1)
    blocks = v.reshape(v.shape[:-1] + (-1, 32))
    amax = np.abs(blocks).max(-1, keepdims=True)
    byte = np.maximum(np.where(amax > 0, np.frexp(amax)[1] - 1 + 127, 0) - down, 1)
    scale = np.exp2(byte - 127.0)
    codes = (blocks / scale).astype(np.float32).astype(dtype).astype(np.float64)
    return np.moveaxis((codes * scale).reshape(v.shape), -1, axis)


WIDE = False


def mx_kscale(k):
    if not WIDE:
        return np.ones(k)
    levels = np.array([10, -10, 5, -5, 0])
    if k % 512:
        return np.exp2(np.random.permutation(np.resize(levels, k // 32))).repeat(32)
    a = np.empty((k // 512, 16))
    for p in range(k // 512):
        a[p, :8] = np.random.permutation(np.resize(levels, 8))
        for g in range(8):
            far = levels[np.abs(levels - a[p, g]) >= 10]
            a[p, g + 8] = far[np.random.randint(len(far))]
    return np.exp2(a.ravel()).repeat(32)


def f64(x):
    return np.asarray(x).astype(np.float64)


def striped(idx):
    return np.tile(idx.reshape(-1, 16).T, (8, 1)).astype(np.uint16)


def unstriped(offs):
    return offs[:16].T.reshape(-1).astype(np.int64)


E2M1 = np.array([0.0, 0.5, 1.0, 1.5, 2.0, 3.0, 4.0, 6.0, -0.0, -0.5, -1.0, -1.5, -2.0, -3.0, -4.0, -6.0])


def pack_weight(w, fmt):
    k, n = w.shape
    w = f64(np.asarray(w, np.float32).astype(ml_dtypes.bfloat16)).reshape(k // 32, 32, n)
    amax = np.abs(w).max(1)
    if fmt == "e4m3":
        byte = np.frexp(amax)[1] - 1 + 127 - 7
    else:
        mant, ex = np.frexp(amax / 6.0)
        byte = np.where(mant > 0.5, ex, ex - 1) + 127
    byte = np.clip(np.where(amax > 0, byte, 1), 1, 254)
    scaled = (w * np.exp2(127.0 - byte)[:, None, :]).reshape(k, n).astype(np.float32)
    by_word = np.ascontiguousarray(scaled.reshape(k // 512, 128, 4, n).transpose(0, 1, 3, 2))
    if fmt == "e4m3":
        words = by_word.astype(ml_dtypes.float8_e4m3fn).view(np.uint8)
    else:
        c = by_word.astype(ml_dtypes.float4_e2m1fn).view(np.uint8) & 0xF
        words = (c[..., 0::2] | (c[..., 1::2] << 4)).reshape(k // 512, 128, 2 * n)
    return np.ascontiguousarray(words), np.ascontiguousarray(byte.astype(np.uint8).reshape(k // 512, 16, n))


def unpack_weight(words, scales, fmt):
    g, _, n = scales.shape
    words = np.ascontiguousarray(words).reshape(g, 128, n, -1)
    if fmt == "e4m3":
        vals = words.view(ml_dtypes.float8_e4m3fn).astype(np.float64)
    else:
        nib = np.empty((g, 128, n, 4), np.uint8)
        nib[..., 0::2] = words & 0xF
        nib[..., 1::2] = words >> 4
        vals = E2M1[nib]
    vals = vals * np.repeat(np.exp2(scales.astype(np.float64) - 127.0), 8, axis=1)[..., None]
    return vals.transpose(0, 1, 3, 2).reshape(g * 512, n)


def gelu(v):
    return 0.5 * v * (1.0 + np.tanh(np.sqrt(2.0 / np.pi) * (v + 0.044715 * v**3)))


K, T, E, C, N = 1536, 1280, 8, 256, 128
PAD = 32


def by_expert(wq, xq):
    return np.concatenate([wq[e].T @ xq[:, e * C:(e + 1) * C] for e in range(E)], axis=1)


def setup_inputs():
    n = np.random.standard_normal
    s = mx_kscale(K)[:, None]
    first = np.random.permutation(np.repeat(np.arange(E), T // E))
    second = (first + 1 + np.random.permutation(np.repeat(np.arange(E - 1), -(-T // (E - 1)))[:T])) % E
    while np.bincount(second, minlength=E).max() != T // E:
        load = np.bincount(second, minlength=E); hi, lo = int(load.argmax()), int(load.argmin())
        t = np.flatnonzero((second == hi) & (first != lo))[0]; second[t] = lo
    slot_token = np.empty(E * C, np.int64); pos = np.empty((2, T), np.int64); fill = np.zeros(E, np.int64)
    place = np.stack([np.random.permutation(C) for _ in range(E)])
    for r, deal in enumerate((first, second)):
        for t in np.random.permutation(T):
            e = deal[t]
            if fill[e] < C: j = e * C + place[e, fill[e]]; fill[e] += 1; slot_token[j] = t; pos[r, t] = j
            else: pos[r, t] = E * C + t % PAD
    g = np.random.uniform(0.2, 0.8, T)
    w = [pack_weight(m, "e2m1") for m in n((E, K, N)) / np.sqrt(K) / s[None]]
    return {
        "xT": (n((K, T)) * s).astype(np.float32),
        "w_words": np.stack([m[0] for m in w]),
        "w_scales": np.stack([m[1] for m in w]),
        "b": (0.3 * n((N, E))).astype(np.float32),
        "gate": np.stack([np.tile(g, (N, 1)), np.tile(1.0 - g, (N, 1))]).astype(np.float32),
        "offs": striped(slot_token),
        "pos1": striped(pos[0]),
        "pos2": striped(pos[1]),
    }


def reference(xT, w_words, w_scales, b, gate, offs, pos1, pos2):
    idx = unstriped(offs)
    w = np.stack([unpack_weight(w_words[e], w_scales[e], "e2m1") for e in range(E)])
    xq = mxq(f64(xT)[:, idx], 0, "e4m3")
    y = by_expert(w, xq)
    y = gelu(y + np.repeat(f64(b), C, axis=1))
    y = np.concatenate([y, np.zeros((N, PAD))], axis=1)
    return f64(gate[0]) * y[:, unstriped(pos1)] + f64(gate[1]) * y[:, unstriped(pos2)]

@@ -1,0 +1,182 @@
+from contextlib import ExitStack
+
+import concourse.mybir as mybir
+
+K, T, E, C, N = 1536, 1280, 8, 256, 128
+S = E * C
+PAD = 32
+P = 128
+PACK = 4
+PASSES = K // (P * PACK)
+FLOPS = 2 * K * N * S
+
+F32 = mybir.dt.float32
+BF16 = mybir.dt.bfloat16
+U32 = mybir.dt.uint32
+I32 = mybir.dt.int32
+U16 = mybir.dt.uint16
+U8 = mybir.dt.uint8
+FP8X4 = mybir.dt.float8_e4m3fn_x4
+FP4X4 = mybir.dt.float4_e2m1fn_x4
+MULT = mybir.AluOpType.mult
+ADD = mybir.AluOpType.add
+COPY = mybir.ActivationFunctionType.Copy
+GELU = mybir.ActivationFunctionType.Gelu_apprx_tanh
+
+BLOCKS = (
+    ((0, 512, 256), (512, 512, 256), (1024, 256, 128)),
+    ((0, 256, 0), (256, 512, 0), (768, 512, 0)),
+    ((0, 512, 0), (512, 512, 0), (1024, 256, 128)),
+)
+PLANE_ROW = (0, 4, 8)
+SLOT_CUTS = (0, 768, 1536, 2048)
+LAST_CUTS = (0, 640, 1280, 1792, 2048)
+TOKEN_CUTS = (0, 640, 1024, 1280)
+
+
+def tile_moe_cap2_lin_gelu_kernel(tc, xT, w_words, w_scales, b, gate, offs, pos1, pos2, out):
+    nc = tc.nc
+    with ExitStack() as ctx:
+        keep = ctx.enter_context(tc.tile_pool(name="keep", bufs=1))
+        psum = ctx.enter_context(tc.psum_pool(name="psum", bufs=8))
+
+        offs_sb = keep.tile([P, S // 16], U16, name="offs_sb")
+        pos1_sb = keep.tile([P, T // 16], U16, name="pos1_sb")
+        pos2_sb = keep.tile([P, T // 16], U16, name="pos2_sb")
+        bias = keep.tile([P, E], F32, name="bias")
+        planes = keep.tile([P, T], U8, name="planes", align_bytes=64)
+        w_sb = keep.tile([P, E * PASSES, 2 * N], U8, name="w_sb", align_bytes=64)
+        ws_sb = keep.tile([P, E * PASSES, N], U8, name="ws_sb", align_bytes=64)
+        y = keep.tile([P, S + PAD], F32, name="y")
+        g0 = keep.tile([P, T], F32, name="g0")
+        g1 = keep.tile([P, T], F32, name="g1")
+        warm = keep.tile([P, 8], F32, name="warm")
+        warmed = keep.tile([P, 8], F32, name="warmed")
+
+        nc.gpsimd.memset(planes[:], 0)
+        nc.gpsimd.memset(warm[:], 0.0)
+        nc.gpsimd.memset(y[:, S:], 0.0)
+        nc.gpsimd.memset(ws_sb[:].rearrange("p g n -> p (g n)").bitcast(I32), 0)
+        nc.scalar.activation(warmed[:], warm[:], GELU)
+
+        raw = []
+        for g in range(PASSES):
+            rows = xT[g * P * PACK:(g + 1) * P * PACK, :].rearrange("(p j) t -> p j t", j=PACK)
+            raw.append([])
+            for c, (t0, width, v) in enumerate(BLOCKS[g]):
+                piece = keep.tile([P, PACK, width], F32, name=f"raw{g}_{c}")
+                nc.sync.dma_start(piece[:], rows[:, :, t0:t0 + width])
+                raw[g].append(piece)
+            if g == 0:
+                nc.sync.dma_start(offs_sb[:], offs)
+        nc.sync.dma_start(w_sb[:].rearrange("p g n -> p g n").bitcast(I32), w_words.rearrange("e a p n -> p (e a) n").bitcast(I32))
+        for q in range(4):
+            nc.sync.dma_start(ws_sb[32 * q:32 * q + 4, :, :].bitcast(I32), w_scales[:, :, 4 * q:4 * q + 4, :].rearrange("e a q n -> q (e a) n").bitcast(I32))
+        nc.sync.dma_start(bias[:], b)
+        nc.sync.dma_start(pos1_sb[:], pos1)
+        nc.sync.dma_start(pos2_sb[:], pos2)
+        nc.sync.dma_start(g0[:], gate[0])
+        nc.sync.dma_start(g1[:], gate[1])
+
+        words = [keep.tile([P, T], U32, name=f"words{g}", align_bytes=64) for g in range(PASSES)]
+        slot_words = [keep.tile([P, S], U32, name=f"slot_words{g}", align_bytes=64) for g in range(PASSES)]
+        slot_planes = keep.tile([P, S], U8, name="slot_planes", align_bytes=64)
+        moved = [slot_planes] + [keep.tile([P, S], U8, name=f"moved{g}", align_bytes=64) for g in range(1, PASSES)]
+
+        def gather_words(g, a, z):
+            nc.vector.tensor_copy(slot_words[g][:, a:z], words[g][:].indirect(offs_sb[:, a // 16:z // 16]))
+
+        for g in range(PASSES):
+            k = PLANE_ROW[g]
+            for c, (t0, width, v) in enumerate(BLOCKS[g]):
+                mixed = keep.tile([P, width, PACK], BF16, name=f"mixed{g}_{c}", align_bytes=64)
+                src = raw[g][c][:]
+                nc.scalar.activation(
+                    mixed[:, v:, :].rearrange("p (c i) j -> p c j i", i=4), src[:, :, v:].rearrange("p j (c i) -> p c j i", i=4), COPY
+                )
+                if v > 0:
+                    nc.vector.tensor_copy(
+                        mixed[:, :v, :].rearrange("p (c i) j -> p c j i", i=4), src[:, :, :v].rearrange("p j (c i) -> p c j i", i=4)
+                    )
+                nc.vector.quantize_mx(
+                    out=words[g][:, t0:t0 + width].bitcast(FP8X4),
+                    scales=planes[k:P, t0:t0 + width],
+                    in_=mixed[:].rearrange("p t j -> p (t j)"),
+                )
+            if g < PASSES - 1:
+                for a, z in zip(SLOT_CUTS, SLOT_CUTS[1:]):
+                    gather_words(g, a, z)
+
+        for a, z, moves in ((0, 640, None), (640, 1280, (0, 1280)), (1280, 2048, (1280, 2048))):
+            nc.vector.tensor_copy(slot_planes[:, a:z], planes[:].indirect(offs_sb[:, a // 16:z // 16]))
+            if moves:
+                m, n = moves
+                for g in (1, 2):
+                    k = PLANE_ROW[g]
+                    for r, rows in ((0, 64), (64, 32), (96, 16)):
+                        nc.sync.dma_start(moved[g][r:r + rows, m:n].bitcast(I32), slot_planes[r + k:r + k + rows, m:n].bitcast(I32))
+
+        for a, z in zip(LAST_CUTS, LAST_CUTS[1:]):
+            gather_words(PASSES - 1, a, z)
+
+        def multiply(acc, e, h, g):
+            s0 = e * C + h * P
+            nc.tensor.matmul_mx(
+                out=acc[:, h * P:(h + 1) * P],
+                lhsT=w_sb[:, e * PASSES + g, :].bitcast(FP4X4),
+                lhsT_scale=ws_sb[:, e * PASSES + g, :],
+                rhs=slot_words[g][:, s0:s0 + P].bitcast(FP8X4),
+                rhs_scale=moved[g][:, s0:s0 + P],
+                start=(g == 0),
+                stop=(g == PASSES - 1),
+            )
+
+        def finish(acc, e, a, z):
+            nc.scalar.activation(y[:, e * C + a:e * C + z], acc[:, a:z], GELU, bias=bias[:, e:e + 1])
+
+        accs = [psum.tile([P, C], F32, name="acc") for e in range(E)]
+        for e in range(E):
+            multiply(accs[e], e, 0, 0)
+        for e in range(5):
+            multiply(accs[e], e, 0, 1)
+        for e in range(E - 1):
+            if e >= 5:
+                multiply(accs[e], e, 0, 1)
+            multiply(accs[e], e, 0, 2)
+            for g in range(PASSES):
+                multiply(accs[e], e, 1, g)
+            finish(accs[e], e, 0, C)
+        e = E - 1
+        extra = psum.tile([P, C], F32, name="acc")
+        multiply(accs[e], e, 0, 1)
+        multiply(extra, e, 1, 0)
+        multiply(extra, e, 1, 1)
+        multiply(accs[e], e, 0, 2)
+        finish(accs[e], e, 0, P)
+        multiply(extra, e, 1, 2)
+        finish(extra, e, P, C)
+
+        parts = list(zip(TOKEN_CUTS, TOKEN_CUTS[1:]))
+        lists = (pos1_sb, pos2_sb)
+        gates = (g0, g1)
+        picked = [[keep.tile([P, z - a], F32, name=f"picked{r}_{a}") for r in range(2)] for a, z in parts]
+
+        def pick(i, r):
+            a, z = parts[i]
+            nc.vector.tensor_tensor(picked[i][r][:], y[:].indirect(lists[r][:, a // 16:z // 16]), gates[r][:, a:z], MULT)
+
+        def combine(i):
+            a, z = parts[i]
+            res = keep.tile([P, z - a], F32, name=f"res{i}")
+            nc.vector.tensor_tensor(res[:], picked[i][0][:], picked[i][1][:], ADD)
+            nc.sync.dma_start(out[:, a:z], res[:])
+
+        pick(0, 0)
+        pick(0, 1)
+        pick(1, 0)
+        combine(0)
+        pick(1, 1)
+        pick(2, 0)
+        pick(2, 1)
+        combine(1)
+        combine(2)

@@ -24,9 +24,9 @@ COPY = mybir.ActivationFunctionType.Copy
 GELU = mybir.ActivationFunctionType.Gelu_apprx_tanh
 
 BLOCKS = (
-    ((0, 512, 256), (512, 512, 256), (1024, 256, 128)),
-    ((0, 256, 0), (256, 512, 0), (768, 512, 0)),
-    ((0, 512, 0), (512, 512, 0), (1024, 256, 128)),
+    (((256, 128),), ((256, 128),), ((256, 128),), ((256, 128),), ((256, 128),)),
+    (((256, 0), (256, 0)), ((256, 0), (256, 0)), ((256, 0),)),
+    (((256, 0), (256, 0)), ((256, 0), (256, 0)), ((256, 0),)),
 )
 PLANE_ROW = (0, 4, 8)
 SLOT_CUTS = (0, 768, 1536, 2048)
@@ -62,13 +62,16 @@ def tile_moe_cap2_lin_gelu_kernel(tc, xT, w_words, w_scales, b, gate, offs, pos1
         raw = []
         for g in range(PASSES):
             rows = xT[g * P * PACK:(g + 1) * P * PACK, :].rearrange("(p j) t -> p j t", j=PACK)
-            raw.append([])
-            for c, (t0, width, v) in enumerate(BLOCKS[g]):
-                piece = keep.tile([P, PACK, width], F32, name=f"raw{g}_{c}")
-                nc.sync.dma_start(piece[:], rows[:, :, t0:t0 + width])
-                raw[g].append(piece)
-            if g == 0:
-                nc.sync.dma_start(offs_sb[:], offs)
+            raw.append({})
+            t0 = 0
+            for block in BLOCKS[g]:
+                for width, v in block:
+                    piece = keep.tile([P, PACK, width], F32, name=f"raw{g}_{t0}")
+                    nc.sync.dma_start(piece[:], rows[:, :, t0:t0 + width])
+                    raw[g][t0] = piece
+                    if g == 0 and t0 == 0:
+                        nc.sync.dma_start(offs_sb[:], offs)
+                    t0 = t0 + width
         nc.sync.dma_start(w_sb[:].rearrange("p g n -> p g n").bitcast(I32), w_words.rearrange("e a p n -> p (e a) n").bitcast(I32))
         for q in range(4):
             nc.sync.dma_start(ws_sb[32 * q:32 * q + 4, :, :].bitcast(I32), w_scales[:, :, 4 * q:4 * q + 4, :].rearrange("e a q n -> q (e a) n").bitcast(I32))
@@ -88,21 +91,29 @@ def tile_moe_cap2_lin_gelu_kernel(tc, xT, w_words, w_scales, b, gate, offs, pos1
 
         for g in range(PASSES):
             k = PLANE_ROW[g]
-            for c, (t0, width, v) in enumerate(BLOCKS[g]):
-                mixed = keep.tile([P, width, PACK], BF16, name=f"mixed{g}_{c}", align_bytes=64)
-                src = raw[g][c][:]
-                nc.scalar.activation(
-                    mixed[:, v:, :].rearrange("p (c i) j -> p c j i", i=4), src[:, :, v:].rearrange("p j (c i) -> p c j i", i=4), COPY
-                )
-                if v > 0:
-                    nc.vector.tensor_copy(
-                        mixed[:, :v, :].rearrange("p (c i) j -> p c j i", i=4), src[:, :, :v].rearrange("p j (c i) -> p c j i", i=4)
+            t0 = 0
+            for block in BLOCKS[g]:
+                first, total = t0, sum(width for width, v in block)
+                mixed = keep.tile([P, total, PACK], BF16, name=f"mixed{g}_{t0}", align_bytes=64)
+                for width, v in block:
+                    src = raw[g][t0][:]
+                    dst = mixed[:, t0 - first:t0 - first + width, :]
+                    nc.scalar.activation(
+                        dst[:, v:, :].rearrange("p (c i) j -> p c j i", i=4), src[:, :, v:].rearrange("p j (c i) -> p c j i", i=4), COPY
                     )
-                nc.vector.quantize_mx(
-                    out=words[g][:, t0:t0 + width].bitcast(FP8X4),
-                    scales=planes[k:P, t0:t0 + width],
-                    in_=mixed[:].rearrange("p t j -> p (t j)"),
-                )
+                    if v > 0:
+                        nc.vector.tensor_copy(
+                            dst[:, :v, :].rearrange("p (c i) j -> p c j i", i=4), src[:, :, :v].rearrange("p j (c i) -> p c j i", i=4)
+                        )
+                    t0 = t0 + width
+                halves = 2 if g == 0 and t0 == T else 1
+                for h in reversed(range(halves)):
+                    a, z = h * total // halves, (h + 1) * total // halves
+                    nc.vector.quantize_mx(
+                        out=words[g][:, first + a:first + z].bitcast(FP8X4),
+                        scales=planes[k:P, first + a:first + z],
+                        in_=mixed[:, a:z, :].rearrange("p t j -> p (t j)"),
+                    )
             if g < PASSES - 1:
                 for a, z in zip(SLOT_CUTS, SLOT_CUTS[1:]):
                     gather_words(g, a, z)

@@ -1,6 +1,7 @@
 from contextlib import ExitStack
 
 import concourse.mybir as mybir
+from concourse.masks import make_identity
 
 K, T, E, C, N = 1536, 1280, 8, 256, 128
 S = E * C
@@ -48,16 +49,18 @@ def tile_moe_cap2_lin_gelu_kernel(tc, xT, w_words, w_scales, b, gate, offs, pos1
         w_sb = keep.tile([P, E * PASSES, 2 * N], U8, name="w_sb", align_bytes=64)
         ws_sb = keep.tile([P, E * PASSES, N], U8, name="ws_sb", align_bytes=64)
         y = keep.tile([P, S + PAD], F32, name="y")
-        g0 = keep.tile([P, T], F32, name="g0")
-        g1 = keep.tile([P, T], F32, name="g1")
+        gate_rows = keep.tile([P, P], F32, name="gate_rows")
+        ident = keep.tile([P, P], F32, name="ident")
         warm = keep.tile([P, 8], F32, name="warm")
         warmed = keep.tile([P, 8], F32, name="warmed")
 
-        nc.gpsimd.memset(planes[:], 0)
         nc.gpsimd.memset(warm[:], 0.0)
-        nc.gpsimd.memset(y[:, S:], 0.0)
-        nc.gpsimd.memset(ws_sb[:].rearrange("p g n -> p (g n)").bitcast(I32), 0)
         nc.scalar.activation(warmed[:], warm[:], GELU)
+        nc.vector.memset(ws_sb[:].rearrange("p g n -> p (g n)").bitcast(I32), 0)
+        nc.vector.memset(gate_rows[:], 0.0)
+        nc.vector.memset(planes[:].bitcast(I32), 0)
+        nc.vector.memset(y[:, S:], 0.0)
+        make_identity(nc, ident[:])
 
         raw = []
         for g in range(PASSES):
@@ -71,15 +74,16 @@ def tile_moe_cap2_lin_gelu_kernel(tc, xT, w_words, w_scales, b, gate, offs, pos1
                     raw[g][t0] = piece
                     if g == 0 and t0 == 0:
                         nc.sync.dma_start(offs_sb[:], offs)
+                    if g == 0 and t0 == 768:
+                        for r in range(2):
+                            nc.sync.dma_start(gate_rows[r * T // P:(r + 1) * T // P, :], gate[r, 0, :].rearrange("(c p) -> c p", p=P))
                     t0 = t0 + width
-        nc.sync.dma_start(w_sb[:].rearrange("p g n -> p g n").bitcast(I32), w_words.rearrange("e a p n -> p (e a) n").bitcast(I32))
-        for q in range(4):
-            nc.sync.dma_start(ws_sb[32 * q:32 * q + 4, :, :].bitcast(I32), w_scales[:, :, 4 * q:4 * q + 4, :].rearrange("e a q n -> q (e a) n").bitcast(I32))
         nc.sync.dma_start(bias[:], b)
         nc.sync.dma_start(pos1_sb[:], pos1)
         nc.sync.dma_start(pos2_sb[:], pos2)
-        nc.sync.dma_start(g0[:], gate[0])
-        nc.sync.dma_start(g1[:], gate[1])
+        for q in range(4):
+            nc.sync.dma_start(ws_sb[32 * q:32 * q + 4, :, :].bitcast(I32), w_scales[:, :, 4 * q:4 * q + 4, :].rearrange("e a q n -> q (e a) n").bitcast(I32))
+        nc.sync.dma_start(w_sb[:].rearrange("p g n -> p g n").bitcast(I32), w_words.rearrange("e a p n -> p (e a) n").bitcast(I32))
 
         words = [keep.tile([P, T], U32, name=f"words{g}", align_bytes=64) for g in range(PASSES)]
         slot_words = [keep.tile([P, S], U32, name=f"slot_words{g}", align_bytes=64) for g in range(PASSES)]
@@ -117,6 +121,19 @@ def tile_moe_cap2_lin_gelu_kernel(tc, xT, w_words, w_scales, b, gate, offs, pos1
             if g < PASSES - 1:
                 for a, z in zip(SLOT_CUTS, SLOT_CUTS[1:]):
                     gather_words(g, a, z)
+            if g == 0:
+                turned = psum.tile([P, P], F32, name="acc")
+                nc.tensor.transpose(turned[:], gate_rows[:], ident[:])
+                gate_cols = keep.tile([P, 2 * T // P], F32, name="raw0_1024")
+                nc.vector.tensor_copy(gate_cols[:], turned[:, :2 * T // P])
+                spreads = [psum.tile([P, 512], F32, name="acc") for bank in range(2 * T // 512)]
+                for col in range(2 * T // P):
+                    c = col % 4
+                    nc.tensor.transpose(spreads[col // 4][:, c * P:(c + 1) * P], gate_cols[:, col:col + 1].to_broadcast([P, P]), ident[:])
+
+        gates = keep.tile([P, 2 * T], F32, name="raw2_1024")
+        for bank, spread in enumerate(spreads):
+            nc.scalar.copy(gates[:, 512 * bank:512 * (bank + 1)], spread[:])
 
         for a, z, moves in ((0, 640, None), (640, 1280, (0, 1280)), (1280, 2048, (1280, 2048))):
             nc.vector.tensor_copy(slot_planes[:, a:z], planes[:].indirect(offs_sb[:, a // 16:z // 16]))
@@ -169,12 +186,11 @@ def tile_moe_cap2_lin_gelu_kernel(tc, xT, w_words, w_scales, b, gate, offs, pos1
 
         parts = list(zip(TOKEN_CUTS, TOKEN_CUTS[1:]))
         lists = (pos1_sb, pos2_sb)
-        gates = (g0, g1)
         picked = [[keep.tile([P, z - a], F32, name=f"picked{r}_{a}") for r in range(2)] for a, z in parts]
 
         def pick(i, r):
             a, z = parts[i]
-            nc.vector.tensor_tensor(picked[i][r][:], y[:].indirect(lists[r][:, a // 16:z // 16]), gates[r][:, a:z], MULT)
+            nc.vector.tensor_tensor(picked[i][r][:], y[:].indirect(lists[r][:, a // 16:z // 16]), gates[:, r * T + a:r * T + z], MULT)
 
         def combine(i):
             a, z = parts[i]

@@ -25,14 +25,14 @@ COPY = mybir.ActivationFunctionType.Copy
 GELU = mybir.ActivationFunctionType.Gelu_apprx_tanh
 
 BLOCKS = (
-    (((256, 128),), ((256, 128),), ((256, 128),), ((256, 128),), ((256, 128),)),
+    (((256, 128),), ((256, 128),), ((256, 128),), ((256, 128),), ((128, 0),), ((128, 128),)),
     (((256, 0), (256, 0)), ((256, 0), (256, 0)), ((256, 0),)),
     (((256, 0), (256, 0)), ((256, 0), (256, 0)), ((256, 0),)),
 )
 PLANE_ROW = (0, 4, 8)
 SLOT_CUTS = (0, 768, 1536, 2048)
 LAST_CUTS = (0, 640, 1280, 1792, 2048)
-TOKEN_CUTS = (0, 640, 1024, 1280)
+TOKEN_CUTS = (0, 256, 512, 896, 1152, 1280)
 
 
 def tile_moe_cap2_lin_gelu_kernel(tc, xT, w_words, w_scales, b, gate, offs, pos1, pos2, out):
@@ -66,6 +66,10 @@ def tile_moe_cap2_lin_gelu_kernel(tc, xT, w_words, w_scales, b, gate, offs, pos1
         for g in range(PASSES):
             rows = xT[g * P * PACK:(g + 1) * P * PACK, :].rearrange("(p j) t -> p j t", j=PACK)
             raw.append({})
+            if g == PASSES - 1:
+                nc.sync.dma_start(bias[:], b)
+                nc.sync.dma_start(pos1_sb[:], pos1)
+                nc.sync.dma_start(pos2_sb[:], pos2)
             t0 = 0
             for block in BLOCKS[g]:
                 for width, v in block:
@@ -78,9 +82,6 @@ def tile_moe_cap2_lin_gelu_kernel(tc, xT, w_words, w_scales, b, gate, offs, pos1
                         for r in range(2):
                             nc.sync.dma_start(gate_rows[r * T // P:(r + 1) * T // P, :], gate[r, 0, :].rearrange("(c p) -> c p", p=P))
                     t0 = t0 + width
-        nc.sync.dma_start(bias[:], b)
-        nc.sync.dma_start(pos1_sb[:], pos1)
-        nc.sync.dma_start(pos2_sb[:], pos2)
         for q in range(4):
             nc.sync.dma_start(ws_sb[32 * q:32 * q + 4, :, :].bitcast(I32), w_scales[:, :, 4 * q:4 * q + 4, :].rearrange("e a q n -> q (e a) n").bitcast(I32))
         nc.sync.dma_start(w_sb[:].rearrange("p g n -> p g n").bitcast(I32), w_words.rearrange("e a p n -> p (e a) n").bitcast(I32))
@@ -102,29 +103,27 @@ def tile_moe_cap2_lin_gelu_kernel(tc, xT, w_words, w_scales, b, gate, offs, pos1
                 for width, v in block:
                     src = raw[g][t0][:]
                     dst = mixed[:, t0 - first:t0 - first + width, :]
-                    nc.scalar.activation(
-                        dst[:, v:, :].rearrange("p (c i) j -> p c j i", i=4), src[:, :, v:].rearrange("p j (c i) -> p c j i", i=4), COPY
-                    )
+                    if v < width:
+                        nc.scalar.activation(
+                            dst[:, v:, :].rearrange("p (c i) j -> p c j i", i=4), src[:, :, v:].rearrange("p j (c i) -> p c j i", i=4), COPY
+                        )
                     if v > 0:
                         nc.vector.tensor_copy(
                             dst[:, :v, :].rearrange("p (c i) j -> p c j i", i=4), src[:, :, :v].rearrange("p j (c i) -> p c j i", i=4)
                         )
                     t0 = t0 + width
-                halves = 2 if g == 0 and t0 == T else 1
-                for h in reversed(range(halves)):
-                    a, z = h * total // halves, (h + 1) * total // halves
-                    nc.vector.quantize_mx(
-                        out=words[g][:, first + a:first + z].bitcast(FP8X4),
-                        scales=planes[k:P, first + a:first + z],
-                        in_=mixed[:, a:z, :].rearrange("p t j -> p (t j)"),
-                    )
+                nc.vector.quantize_mx(
+                    out=words[g][:, first:first + total].bitcast(FP8X4),
+                    scales=planes[k:P, first:first + total],
+                    in_=mixed[:].rearrange("p t j -> p (t j)"),
+                )
             if g < PASSES - 1:
                 for a, z in zip(SLOT_CUTS, SLOT_CUTS[1:]):
                     gather_words(g, a, z)
             if g == 0:
                 turned = psum.tile([P, P], F32, name="acc")
                 nc.tensor.transpose(turned[:], gate_rows[:], ident[:])
-                gate_cols = keep.tile([P, 2 * T // P], F32, name="raw0_1024")
+                gate_cols = keep.tile([P, 2 * T // P], F32, name="raw0_1152")
                 nc.vector.tensor_copy(gate_cols[:], turned[:, :2 * T // P])
                 spreads = [psum.tile([P, 512], F32, name="acc") for bank in range(2 * T // 512)]
                 for col in range(2 * T // P):
@@ -198,12 +197,37 @@ def tile_moe_cap2_lin_gelu_kernel(tc, xT, w_words, w_scales, b, gate, offs, pos1
             nc.vector.tensor_tensor(res[:], picked[i][0][:], picked[i][1][:], ADD)
             nc.sync.dma_start(out[:, a:z], res[:])
 
-        pick(0, 0)
-        pick(0, 1)
-        pick(1, 0)
-        combine(0)
-        pick(1, 1)
+        turned_sums = {}
+
+        def add_turned(i):
+            a, z = parts[i]
+            turned_sums[i] = psum.tile([P, z - a], F32, name="acc")
+            for c in range(0, z - a, P):
+                for r in range(2):
+                    nc.tensor.matmul(turned_sums[i][:, c:c + P], lhsT=picked[i][r][:, c:c + P], rhs=ident[:], is_transpose=True, start=(r == 0), stop=(r == 1))
+
+        def turn_back(i, tag):
+            a, z = parts[i]
+            summed = keep.tile([P, z - a], F32, name=tag)
+            nc.scalar.copy(summed[:], turned_sums[i][:])
+            back = psum.tile([P, z - a], F32, name="acc")
+            for c in range(0, z - a, P):
+                nc.tensor.transpose(back[:, c:c + P], summed[:, c:c + P], ident[:])
+            res = keep.tile([P, z - a], F32, name=f"res{i}")
+            nc.scalar.copy(res[:], back[:])
+            nc.sync.dma_start(out[:, a:z], res[:])
+
+        for i in range(2):
+            pick(i, 0)
+            pick(i, 1)
+            add_turned(i)
+            turn_back(i, f"summed{i}")
         pick(2, 0)
         pick(2, 1)
-        combine(1)
+        pick(3, 0)
         combine(2)
+        pick(3, 1)
+        pick(4, 0)
+        pick(4, 1)
+        combine(3)
+        combine(4)

@@ -41,18 +41,18 @@ def tile_moe_cap2_lin_gelu_kernel(tc, xT, w_words, w_scales, b, gate, offs, pos1
         keep = ctx.enter_context(tc.tile_pool(name="keep", bufs=1))
         psum = ctx.enter_context(tc.psum_pool(name="psum", bufs=8))
 
-        offs_sb = keep.tile([P, S // 16], U16, name="offs_sb")
-        pos1_sb = keep.tile([P, T // 16], U16, name="pos1_sb")
-        pos2_sb = keep.tile([P, T // 16], U16, name="pos2_sb")
-        bias = keep.tile([P, E], F32, name="bias")
-        planes = keep.tile([P, T], U8, name="planes", align_bytes=64)
-        w_sb = keep.tile([P, E * PASSES, 2 * N], U8, name="w_sb", align_bytes=64)
-        ws_sb = keep.tile([P, E * PASSES, N], U8, name="ws_sb", align_bytes=64)
-        y = keep.tile([P, S + PAD], F32, name="y")
-        gate_rows = keep.tile([P, P], F32, name="gate_rows")
-        ident = keep.tile([P, P], F32, name="ident")
-        warm = keep.tile([P, 8], F32, name="warm")
-        warmed = keep.tile([P, 8], F32, name="warmed")
+        offs_sb = keep.tile([P, S // 16], U16, name="offs_sb", align_bytes=256)
+        pos1_sb = keep.tile([P, T // 16], U16, name="pos1_sb", align_bytes=256)
+        pos2_sb = keep.tile([P, T // 16], U16, name="pos2_sb", align_bytes=256)
+        bias = keep.tile([P, E], F32, name="bias", align_bytes=256)
+        planes = keep.tile([P, T], U8, name="planes", align_bytes=256)
+        w_sb = keep.tile([P, E * PASSES, 2 * N], U8, name="w_sb", align_bytes=256)
+        ws_sb = keep.tile([P, E * PASSES, N], U8, name="ws_sb", align_bytes=256)
+        y = keep.tile([P, S + PAD], F32, name="y", align_bytes=256)
+        gate_rows = keep.tile([P, P], F32, name="gate_rows", align_bytes=256)
+        ident = keep.tile([P, P], F32, name="ident", align_bytes=256)
+        warm = keep.tile([P, 8], F32, name="warm", align_bytes=256)
+        warmed = keep.tile([P, 8], F32, name="warmed", align_bytes=256)
 
         nc.gpsimd.memset(warm[:], 0.0)
         nc.scalar.activation(warmed[:], warm[:], GELU)
@@ -73,7 +73,7 @@ def tile_moe_cap2_lin_gelu_kernel(tc, xT, w_words, w_scales, b, gate, offs, pos1
             t0 = 0
             for block in BLOCKS[g]:
                 for width, v in block:
-                    piece = keep.tile([P, PACK, width], F32, name=f"raw{g}_{t0}")
+                    piece = keep.tile([P, PACK, width], F32, name=f"raw{g}_{t0}", align_bytes=256)
                     nc.sync.dma_start(piece[:], rows[:, :, t0:t0 + width])
                     raw[g][t0] = piece
                     if g == 0 and t0 == 0:
@@ -86,10 +86,10 @@ def tile_moe_cap2_lin_gelu_kernel(tc, xT, w_words, w_scales, b, gate, offs, pos1
             nc.sync.dma_start(ws_sb[32 * q:32 * q + 4, :, :].bitcast(I32), w_scales[:, :, 4 * q:4 * q + 4, :].rearrange("e a q n -> q (e a) n").bitcast(I32))
         nc.sync.dma_start(w_sb[:].rearrange("p g n -> p g n").bitcast(I32), w_words.rearrange("e a p n -> p (e a) n").bitcast(I32))
 
-        words = [keep.tile([P, T], U32, name=f"words{g}", align_bytes=64) for g in range(PASSES)]
-        slot_words = [keep.tile([P, S], U32, name=f"slot_words{g}", align_bytes=64) for g in range(PASSES)]
-        slot_planes = keep.tile([P, S], U8, name="slot_planes", align_bytes=64)
-        moved = [slot_planes] + [keep.tile([P, S], U8, name=f"moved{g}", align_bytes=64) for g in range(1, PASSES)]
+        words = [keep.tile([P, T], U32, name=f"words{g}", align_bytes=256) for g in range(PASSES)]
+        slot_words = [keep.tile([P, S], U32, name=f"slot_words{g}", align_bytes=256) for g in range(PASSES)]
+        slot_planes = keep.tile([P, S], U8, name="slot_planes", align_bytes=256)
+        moved = [slot_planes] + [keep.tile([P, S], U8, name=f"moved{g}", align_bytes=256) for g in range(1, PASSES)]
 
         def gather_words(g, a, z):
             nc.vector.tensor_copy(slot_words[g][:, a:z], words[g][:].indirect(offs_sb[:, a // 16:z // 16]))
@@ -99,7 +99,7 @@ def tile_moe_cap2_lin_gelu_kernel(tc, xT, w_words, w_scales, b, gate, offs, pos1
             t0 = 0
             for block in BLOCKS[g]:
                 first, total = t0, sum(width for width, v in block)
-                mixed = keep.tile([P, total, PACK], BF16, name=f"mixed{g}_{t0}", align_bytes=64)
+                mixed = keep.tile([P, total, PACK], BF16, name=f"mixed{g}_{t0}", align_bytes=256)
                 for width, v in block:
                     src = raw[g][t0][:]
                     dst = mixed[:, t0 - first:t0 - first + width, :]
@@ -123,14 +123,14 @@ def tile_moe_cap2_lin_gelu_kernel(tc, xT, w_words, w_scales, b, gate, offs, pos1
             if g == 0:
                 turned = psum.tile([P, P], F32, name="acc")
                 nc.tensor.transpose(turned[:], gate_rows[:], ident[:])
-                gate_cols = keep.tile([P, 2 * T // P], F32, name="raw0_1152")
+                gate_cols = keep.tile([P, 2 * T // P], F32, name="raw0_1152", align_bytes=256)
                 nc.vector.tensor_copy(gate_cols[:], turned[:, :2 * T // P])
                 spreads = [psum.tile([P, 512], F32, name="acc") for bank in range(2 * T // 512)]
                 for col in range(2 * T // P):
                     c = col % 4
                     nc.tensor.transpose(spreads[col // 4][:, c * P:(c + 1) * P], gate_cols[:, col:col + 1].to_broadcast([P, P]), ident[:])
 
-        gates = keep.tile([P, 2 * T], F32, name="raw2_1024")
+        gates = keep.tile([P, 2 * T], F32, name="raw2_1024", align_bytes=256)
         for bank, spread in enumerate(spreads):
             nc.scalar.copy(gates[:, 512 * bank:512 * (bank + 1)], spread[:])
 
@@ -185,7 +185,7 @@ def tile_moe_cap2_lin_gelu_kernel(tc, xT, w_words, w_scales, b, gate, offs, pos1
 
         parts = list(zip(TOKEN_CUTS, TOKEN_CUTS[1:]))
         lists = (pos1_sb, pos2_sb)
-        picked = [[keep.tile([P, z - a], F32, name=f"picked{r}_{a}") for r in range(2)] for a, z in parts]
+        picked = [[keep.tile([P, z - a], F32, name=f"picked{r}_{a}", align_bytes=256) for r in range(2)] for a, z in parts]
 
         def pick(i, r):
             a, z = parts[i]
@@ -193,7 +193,7 @@ def tile_moe_cap2_lin_gelu_kernel(tc, xT, w_words, w_scales, b, gate, offs, pos1
 
         def combine(i):
             a, z = parts[i]
-            res = keep.tile([P, z - a], F32, name=f"res{i}")
+            res = keep.tile([P, z - a], F32, name=f"res{i}", align_bytes=256)
             nc.vector.tensor_tensor(res[:], picked[i][0][:], picked[i][1][:], ADD)
             nc.sync.dma_start(out[:, a:z], res[:])
 
@@ -208,12 +208,12 @@ def tile_moe_cap2_lin_gelu_kernel(tc, xT, w_words, w_scales, b, gate, offs, pos1
 
         def turn_back(i, tag):
             a, z = parts[i]
-            summed = keep.tile([P, z - a], F32, name=tag)
+            summed = keep.tile([P, z - a], F32, name=tag, align_bytes=256)
             nc.scalar.copy(summed[:], turned_sums[i][:])
             back = psum.tile([P, z - a], F32, name="acc")
             for c in range(0, z - a, P):
                 nc.tensor.transpose(back[:, c:c + P], summed[:, c:c + P], ident[:])
-            res = keep.tile([P, z - a], F32, name=f"res{i}")
+            res = keep.tile([P, z - a], F32, name=f"res{i}", align_bytes=256)
             nc.scalar.copy(res[:], back[:])
             nc.sync.dma_start(out[:, a:z], res[:])
 

@@ -30,8 +30,9 @@ BLOCKS = (
     (((256, 0), (256, 0)), ((256, 0), (256, 0)), ((256, 0),)),
 )
 PLANE_ROW = (0, 4, 8)
-SLOT_CUTS = (0, 768, 1536, 2048)
-LAST_CUTS = (0, 640, 1280, 1792, 2048)
+WIDE = 1376
+SLOT_CUTS = (0, 1024, 2048)
+LAST_CUTS = (0, 512, 1024, 1536, 1792, 2048)
 TOKEN_CUTS = (0, 256, 512, 896, 1152, 1280)
 
 
@@ -45,11 +46,11 @@ def tile_moe_cap2_lin_gelu_kernel(tc, xT, w_words, w_scales, b, gate, offs, pos1
         pos1_sb = keep.tile([P, T // 16], U16, name="pos1_sb", align_bytes=256)
         pos2_sb = keep.tile([P, T // 16], U16, name="pos2_sb", align_bytes=256)
         bias = keep.tile([P, E], F32, name="bias", align_bytes=256)
-        planes = keep.tile([P, T], U8, name="planes", align_bytes=256)
+        planes = keep.tile([P, WIDE], U8, name="planes", align_bytes=256)
         w_sb = keep.tile([P, E * PASSES, 2 * N], U8, name="w_sb", align_bytes=256)
         ws_sb = keep.tile([P, E * PASSES, N], U8, name="ws_sb", align_bytes=256)
         y = keep.tile([P, S + PAD], F32, name="y", align_bytes=256)
-        gate_rows = keep.tile([P, P], F32, name="gate_rows", align_bytes=256)
+        gate_rows = keep.tile([P, 2, P], F32, name="gate_rows", align_bytes=256)
         ident = keep.tile([P, P], F32, name="ident", align_bytes=256)
         warm = keep.tile([P, 8], F32, name="warm", align_bytes=256)
         warmed = keep.tile([P, 8], F32, name="warmed", align_bytes=256)
@@ -57,7 +58,7 @@ def tile_moe_cap2_lin_gelu_kernel(tc, xT, w_words, w_scales, b, gate, offs, pos1
         nc.gpsimd.memset(warm[:], 0.0)
         nc.scalar.activation(warmed[:], warm[:], GELU)
         nc.vector.memset(ws_sb[:].rearrange("p g n -> p (g n)").bitcast(I32), 0)
-        nc.vector.memset(gate_rows[:], 0.0)
+        nc.vector.memset(gate_rows[:].rearrange("p r c -> p (r c)"), 0.0)
         nc.vector.memset(planes[:].bitcast(I32), 0)
         nc.vector.memset(y[:, S:], 0.0)
         make_identity(nc, ident[:])
@@ -66,27 +67,27 @@ def tile_moe_cap2_lin_gelu_kernel(tc, xT, w_words, w_scales, b, gate, offs, pos1
         for g in range(PASSES):
             rows = xT[g * P * PACK:(g + 1) * P * PACK, :].rearrange("(p j) t -> p j t", j=PACK)
             raw.append({})
-            if g == PASSES - 1:
-                nc.sync.dma_start(bias[:], b)
-                nc.sync.dma_start(pos1_sb[:], pos1)
-                nc.sync.dma_start(pos2_sb[:], pos2)
             t0 = 0
             for block in BLOCKS[g]:
                 for width, v in block:
                     piece = keep.tile([P, PACK, width], F32, name=f"raw{g}_{t0}", align_bytes=256)
                     nc.sync.dma_start(piece[:], rows[:, :, t0:t0 + width])
                     raw[g][t0] = piece
-                    if g == 0 and t0 == 0:
-                        nc.sync.dma_start(offs_sb[:], offs)
-                    if g == 0 and t0 == 768:
-                        for r in range(2):
-                            nc.sync.dma_start(gate_rows[r * T // P:(r + 1) * T // P, :], gate[r, 0, :].rearrange("(c p) -> c p", p=P))
                     t0 = t0 + width
+            if g == 0:
+                nc.sync.dma_start(offs_sb[:], offs)
+                for a, z in ((0, 8), (8, 10)):
+                    nc.sync.dma_start(gate_rows[a:z, :, :], gate[:, 0, a * P:z * P].rearrange("r (c p) -> c r p", p=P))
+        nc.sync.dma_start(bias[:], b)
+        nc.sync.dma_start(pos1_sb[:], pos1)
+        nc.sync.dma_start(pos2_sb[:], pos2)
         for q in range(4):
             nc.sync.dma_start(ws_sb[32 * q:32 * q + 4, :, :].bitcast(I32), w_scales[:, :, 4 * q:4 * q + 4, :].rearrange("e a q n -> q (e a) n").bitcast(I32))
         nc.sync.dma_start(w_sb[:].rearrange("p g n -> p g n").bitcast(I32), w_words.rearrange("e a p n -> p (e a) n").bitcast(I32))
 
-        words = [keep.tile([P, T], U32, name=f"words{g}", align_bytes=256) for g in range(PASSES)]
+        words = [keep.tile([P, WIDE if g < PASSES - 1 else T], U32, name=f"words{g}", align_bytes=256) for g in range(PASSES)]
+        for g in range(PASSES - 1):
+            nc.vector.memset(words[g][:, T:].bitcast(I32), 0)
         slot_words = [keep.tile([P, S], U32, name=f"slot_words{g}", align_bytes=256) for g in range(PASSES)]
         slot_planes = keep.tile([P, S], U8, name="slot_planes", align_bytes=256)
         moved = [slot_planes] + [keep.tile([P, S], U8, name=f"moved{g}", align_bytes=256) for g in range(1, PASSES)]
@@ -121,10 +122,11 @@ def tile_moe_cap2_lin_gelu_kernel(tc, xT, w_words, w_scales, b, gate, offs, pos1
                 for a, z in zip(SLOT_CUTS, SLOT_CUTS[1:]):
                     gather_words(g, a, z)
             if g == 0:
-                turned = psum.tile([P, P], F32, name="acc")
-                nc.tensor.transpose(turned[:], gate_rows[:], ident[:])
+                turned = psum.tile([P, 2, P], F32, name="acc")
+                for r in range(2):
+                    nc.tensor.transpose(turned[:, r, :], gate_rows[:, r, :], ident[:])
                 gate_cols = keep.tile([P, 2 * T // P], F32, name="raw0_1152", align_bytes=256)
-                nc.vector.tensor_copy(gate_cols[:], turned[:, :2 * T // P])
+                nc.vector.tensor_copy(gate_cols[:].rearrange("p (r c) -> p r c", r=2), turned[:, :, :T // P])
                 spreads = [psum.tile([P, 512], F32, name="acc") for bank in range(2 * T // 512)]
                 for col in range(2 * T // P):
                     c = col % 4
@@ -134,14 +136,12 @@ def tile_moe_cap2_lin_gelu_kernel(tc, xT, w_words, w_scales, b, gate, offs, pos1
         for bank, spread in enumerate(spreads):
             nc.scalar.copy(gates[:, 512 * bank:512 * (bank + 1)], spread[:])
 
-        for a, z, moves in ((0, 640, None), (640, 1280, (0, 1280)), (1280, 2048, (1280, 2048))):
+        for a, z in zip(SLOT_CUTS, SLOT_CUTS[1:]):
             nc.vector.tensor_copy(slot_planes[:, a:z], planes[:].indirect(offs_sb[:, a // 16:z // 16]))
-            if moves:
-                m, n = moves
-                for g in (1, 2):
-                    k = PLANE_ROW[g]
-                    for r, rows in ((0, 64), (64, 32), (96, 16)):
-                        nc.sync.dma_start(moved[g][r:r + rows, m:n].bitcast(I32), slot_planes[r + k:r + k + rows, m:n].bitcast(I32))
+            for g in (1, 2):
+                k = PLANE_ROW[g]
+                for r, rows in ((0, 64), (64, 32), (96, 16)):
+                    nc.sync.dma_start(moved[g][r:r + rows, a:z].bitcast(I32), slot_planes[r + k:r + k + rows, a:z].bitcast(I32))
 
         for a, z in zip(LAST_CUTS, LAST_CUTS[1:]):
             gather_words(PASSES - 1, a, z)
@@ -161,27 +161,31 @@ def tile_moe_cap2_lin_gelu_kernel(tc, xT, w_words, w_scales, b, gate, offs, pos1
         def finish(acc, e, a, z):
             nc.scalar.activation(y[:, e * C + a:e * C + z], acc[:, a:z], GELU, bias=bias[:, e:e + 1])
 
-        accs = [psum.tile([P, C], F32, name="acc") for e in range(E)]
-        for e in range(E):
-            multiply(accs[e], e, 0, 0)
-        for e in range(5):
-            multiply(accs[e], e, 0, 1)
-        for e in range(E - 1):
-            if e >= 5:
-                multiply(accs[e], e, 0, 1)
+        def close(e):
             multiply(accs[e], e, 0, 2)
             for g in range(PASSES):
                 multiply(accs[e], e, 1, g)
             finish(accs[e], e, 0, C)
-        e = E - 1
+
+        accs = [psum.tile([P, C], F32, name="acc") for e in range(E)]
+        last = E - 1
+        for e in range(E):
+            multiply(accs[e], e, 0, 0)
+        for e in range(E // 2):
+            multiply(accs[e], e, 0, 1)
+        for e in range(E // 2):
+            close(e)
+        for e in range(E // 2, E):
+            multiply(accs[e], e, 0, 1)
         extra = psum.tile([P, C], F32, name="acc")
-        multiply(accs[e], e, 0, 1)
-        multiply(extra, e, 1, 0)
-        multiply(extra, e, 1, 1)
-        multiply(accs[e], e, 0, 2)
-        finish(accs[e], e, 0, P)
-        multiply(extra, e, 1, 2)
-        finish(extra, e, P, C)
+        multiply(extra, last, 1, 0)
+        multiply(extra, last, 1, 1)
+        for e in range(E // 2, last):
+            close(e)
+        multiply(accs[last], last, 0, 2)
+        finish(accs[last], last, 0, P)
+        multiply(extra, last, 1, 2)
+        finish(extra, last, P, C)
 
         parts = list(zip(TOKEN_CUTS, TOKEN_CUTS[1:]))
         lists = (pos1_sb, pos2_sb)

@@ -26,8 +26,8 @@ GELU = mybir.ActivationFunctionType.Gelu_apprx_tanh
 
 BLOCKS = (
     (((256, 128),), ((256, 128),), ((256, 128),), ((256, 128),), ((128, 0),), ((128, 128),)),
-    (((256, 0), (256, 0)), ((256, 0), (256, 0)), ((256, 0),)),
-    (((256, 0), (256, 0)), ((256, 0), (256, 0)), ((256, 0),)),
+    (((128, 0), (128, 0), (256, 0)), ((256, 0), (256, 0)), ((128, 0),), ((128, 0),)),
+    (((256, 0), (256, 0)), ((256, 0), (256, 0)), ((128, 0),), ((128, 0),)),
 )
 PLANE_ROW = (0, 4, 8)
 WIDE = 1376
@@ -52,15 +52,13 @@ def tile_moe_cap2_lin_gelu_kernel(tc, xT, w_words, w_scales, b, gate, offs, pos1
         y = keep.tile([P, S + PAD], F32, name="y", align_bytes=256)
         gate_rows = keep.tile([P, 2, P], F32, name="gate_rows", align_bytes=256)
         ident = keep.tile([P, P], F32, name="ident", align_bytes=256)
-        warm = keep.tile([P, 8], F32, name="warm", align_bytes=256)
-        warmed = keep.tile([P, 8], F32, name="warmed", align_bytes=256)
+        zeros = keep.tile([P, PAD], F32, name="zeros", align_bytes=256)
 
-        nc.gpsimd.memset(warm[:], 0.0)
-        nc.scalar.activation(warmed[:], warm[:], GELU)
+        nc.gpsimd.memset(zeros[:], 0.0)
+        nc.scalar.activation(y[:, S:], zeros[:], GELU)
         nc.vector.memset(ws_sb[:].rearrange("p g n -> p (g n)").bitcast(I32), 0)
         nc.vector.memset(gate_rows[:].rearrange("p r c -> p (r c)"), 0.0)
         nc.vector.memset(planes[:].bitcast(I32), 0)
-        nc.vector.memset(y[:, S:], 0.0)
         make_identity(nc, ident[:])
 
         raw = []
@@ -132,7 +130,7 @@ def tile_moe_cap2_lin_gelu_kernel(tc, xT, w_words, w_scales, b, gate, offs, pos1
                     c = col % 4
                     nc.tensor.transpose(spreads[col // 4][:, c * P:(c + 1) * P], gate_cols[:, col:col + 1].to_broadcast([P, P]), ident[:])
 
-        gates = keep.tile([P, 2 * T], F32, name="raw2_1024", align_bytes=256)
+        gates = keep.tile([P, 2 * T], F32, name="raw2_1152", align_bytes=256)
         for bank, spread in enumerate(spreads):
             nc.scalar.copy(gates[:, 512 * bank:512 * (bank + 1)], spread[:])
 

@@ -33,7 +33,7 @@ PLANE_ROW = (0, 4, 8)
 WIDE = 1376
 SLOT_CUTS = (0, 1024, 2048)
 LAST_CUTS = (0, 512, 1024, 1536, 1792, 2048)
-TOKEN_CUTS = (0, 256, 512, 896, 1152, 1280)
+TOKEN_CUTS = (0, 256, 384, 896, 1152, 1280)
 
 
 def tile_moe_cap2_lin_gelu_kernel(tc, xT, w_words, w_scales, b, gate, offs, pos1, pos2, out):
@@ -56,7 +56,6 @@ def tile_moe_cap2_lin_gelu_kernel(tc, xT, w_words, w_scales, b, gate, offs, pos1
 
         nc.gpsimd.memset(zeros[:], 0.0)
         nc.scalar.activation(y[:, S:], zeros[:], GELU)
-        nc.vector.memset(ws_sb[:].rearrange("p g n -> p (g n)").bitcast(I32), 0)
         nc.vector.memset(gate_rows[:].rearrange("p r c -> p (r c)"), 0.0)
         nc.vector.memset(planes[:].bitcast(I32), 0)
         make_identity(nc, ident[:])
@@ -116,19 +115,19 @@ def tile_moe_cap2_lin_gelu_kernel(tc, xT, w_words, w_scales, b, gate, offs, pos1
                     scales=planes[k:P, first:first + total],
                     in_=mixed[:].rearrange("p t j -> p (t j)"),
                 )
-            if g < PASSES - 1:
-                for a, z in zip(SLOT_CUTS, SLOT_CUTS[1:]):
-                    gather_words(g, a, z)
-            if g == 0:
+            if g == 1:
                 turned = psum.tile([P, 2, P], F32, name="acc")
                 for r in range(2):
                     nc.tensor.transpose(turned[:, r, :], gate_rows[:, r, :], ident[:])
-                gate_cols = keep.tile([P, 2 * T // P], F32, name="raw0_1152", align_bytes=256)
+                gate_cols = keep.tile([P, 2 * T // P], F32, name="raw1_1152", align_bytes=256)
                 nc.vector.tensor_copy(gate_cols[:].rearrange("p (r c) -> p r c", r=2), turned[:, :, :T // P])
                 spreads = [psum.tile([P, 512], F32, name="acc") for bank in range(2 * T // 512)]
                 for col in range(2 * T // P):
                     c = col % 4
                     nc.tensor.transpose(spreads[col // 4][:, c * P:(c + 1) * P], gate_cols[:, col:col + 1].to_broadcast([P, P]), ident[:])
+            if g < PASSES - 1:
+                for a, z in zip(SLOT_CUTS, SLOT_CUTS[1:]):
+                    gather_words(g, a, z)
 
         gates = keep.tile([P, 2 * T], F32, name="raw2_1152", align_bytes=256)
         for bank, spread in enumerate(spreads):
@@ -138,7 +137,7 @@ def tile_moe_cap2_lin_gelu_kernel(tc, xT, w_words, w_scales, b, gate, offs, pos1
             nc.vector.tensor_copy(slot_planes[:, a:z], planes[:].indirect(offs_sb[:, a // 16:z // 16]))
             for g in (1, 2):
                 k = PLANE_ROW[g]
-                for r, rows in ((0, 64), (64, 32), (96, 16)):
+                for r, rows in ((0, 64), (64, 4), (96, 4)):
                     nc.sync.dma_start(moved[g][r:r + rows, a:z].bitcast(I32), slot_planes[r + k:r + k + rows, a:z].bitcast(I32))
 
         for a, z in zip(LAST_CUTS, LAST_CUTS[1:]):

@@ -27,13 +27,13 @@ GELU = mybir.ActivationFunctionType.Gelu_apprx_tanh
 BLOCKS = (
     (((256, 128),), ((256, 128),), ((256, 128),), ((256, 128),), ((128, 0),), ((128, 128),)),
     (((128, 0), (128, 0), (256, 0)), ((256, 0), (256, 0)), ((128, 0),), ((128, 0),)),
-    (((256, 0), (256, 0)), ((256, 0), (256, 0)), ((128, 0),), ((128, 0),)),
+    (((256, 0), (256, 0)), ((256, 0), (256, 0)), ((128, 0), (128, 0))),
 )
 PLANE_ROW = (0, 4, 8)
 WIDE = 1376
 SLOT_CUTS = (0, 1024, 2048)
 LAST_CUTS = (0, 512, 1024, 1536, 1792, 2048)
-TOKEN_CUTS = (0, 256, 384, 896, 1152, 1280)
+TOKEN_CUTS = (0, 256, 512, 896, 1152, 1280)
 
 
 def tile_moe_cap2_lin_gelu_kernel(tc, xT, w_words, w_scales, b, gate, offs, pos1, pos2, out):
@@ -125,11 +125,14 @@ def tile_moe_cap2_lin_gelu_kernel(tc, xT, w_words, w_scales, b, gate, offs, pos1
                 for col in range(2 * T // P):
                     c = col % 4
                     nc.tensor.transpose(spreads[col // 4][:, c * P:(c + 1) * P], gate_cols[:, col:col + 1].to_broadcast([P, P]), ident[:])
+            if g == 2:
+                held = keep.tile([P, C], U32, name=f"raw{g}_{T - P}", align_bytes=256)
+                nc.vector.tensor_copy(held[:], words[1][:].indirect(offs_sb[:, (S - C) // 16:]))
             if g < PASSES - 1:
-                for a, z in zip(SLOT_CUTS, SLOT_CUTS[1:]):
+                for a, z in ((0, 1024), (1024, S - g * C)):
                     gather_words(g, a, z)
 
-        gates = keep.tile([P, 2 * T], F32, name="raw2_1152", align_bytes=256)
+        gates = keep.tile([P, 2 * T], F32, name="mixed2_1024", align_bytes=256)
         for bank, spread in enumerate(spreads):
             nc.scalar.copy(gates[:, 512 * bank:512 * (bank + 1)], spread[:])
 
@@ -145,11 +148,12 @@ def tile_moe_cap2_lin_gelu_kernel(tc, xT, w_words, w_scales, b, gate, offs, pos1
 
         def multiply(acc, e, h, g):
             s0 = e * C + h * P
+            codes = held[:, h * P:(h + 1) * P] if e == E - 1 and g == 1 else slot_words[g][:, s0:s0 + P]
             nc.tensor.matmul_mx(
                 out=acc[:, h * P:(h + 1) * P],
                 lhsT=w_sb[:, e * PASSES + g, :].bitcast(FP4X4),
                 lhsT_scale=ws_sb[:, e * PASSES + g, :],
-                rhs=slot_words[g][:, s0:s0 + P].bitcast(FP8X4),
+                rhs=codes.bitcast(FP8X4),
                 rhs_scale=moved[g][:, s0:s0 + P],
                 start=(g == 0),
                 stop=(g == PASSES - 1),

@@ -40,7 +40,7 @@ def tile_moe_cap2_lin_gelu_kernel(tc, xT, w_words, w_scales, b, gate, offs, pos1
     nc = tc.nc
     with ExitStack() as ctx:
         keep = ctx.enter_context(tc.tile_pool(name="keep", bufs=1))
-        psum = ctx.enter_context(tc.psum_pool(name="psum", bufs=8))
+        psum = ctx.enter_context(tc.psum_pool(name="psum", bufs=1))
 
         offs_sb = keep.tile([P, S // 16], U16, name="offs_sb", align_bytes=256)
         pos1_sb = keep.tile([P, T // 16], U16, name="pos1_sb", align_bytes=256)
@@ -103,7 +103,7 @@ def tile_moe_cap2_lin_gelu_kernel(tc, xT, w_words, w_scales, b, gate, offs, pos1
                     dst = mixed[:, t0 - first:t0 - first + width, :]
                     if v < width:
                         nc.scalar.activation(
-                            dst[:, v:, :].rearrange("p (c i) j -> p c j i", i=4), src[:, :, v:].rearrange("p j (c i) -> p c j i", i=4), COPY
+                            dst[:, v:, :].rearrange("p (c i) j -> p c j i", i=2), src[:, :, v:].rearrange("p j (c i) -> p c j i", i=2), COPY
                         )
                     if v > 0:
                         nc.vector.tensor_copy(
@@ -116,12 +116,12 @@ def tile_moe_cap2_lin_gelu_kernel(tc, xT, w_words, w_scales, b, gate, offs, pos1
                     in_=mixed[:].rearrange("p t j -> p (t j)"),
                 )
             if g == 1:
-                turned = psum.tile([P, 2, P], F32, name="acc")
+                turned = psum.tile([P, 2, P], F32, name="bank2")
                 for r in range(2):
                     nc.tensor.transpose(turned[:, r, :], gate_rows[:, r, :], ident[:])
                 gate_cols = keep.tile([P, 2 * T // P], F32, name="raw1_1152", align_bytes=256)
                 nc.vector.tensor_copy(gate_cols[:].rearrange("p (r c) -> p r c", r=2), turned[:, :, :T // P])
-                spreads = [psum.tile([P, 512], F32, name="acc") for bank in range(2 * T // 512)]
+                spreads = [psum.tile([P, 512], F32, name=f"bank{3 + bank}") for bank in range(2 * T // 512)]
                 for col in range(2 * T // P):
                     c = col % 4
                     nc.tensor.transpose(spreads[col // 4][:, c * P:(c + 1) * P], gate_cols[:, col:col + 1].to_broadcast([P, P]), ident[:])
@@ -155,38 +155,26 @@ def tile_moe_cap2_lin_gelu_kernel(tc, xT, w_words, w_scales, b, gate, offs, pos1
                 lhsT_scale=ws_sb[:, e * PASSES + g, :],
                 rhs=codes.bitcast(FP8X4),
                 rhs_scale=moved[g][:, s0:s0 + P],
-                start=(g == 0),
-                stop=(g == PASSES - 1),
+                start=(g == 0 and h == 0),
+                stop=(g == PASSES - 1 and h == 1),
             )
 
-        def finish(acc, e, a, z):
-            nc.scalar.activation(y[:, e * C + a:e * C + z], acc[:, a:z], GELU, bias=bias[:, e:e + 1])
+        def both(e, g):
+            for h in range(2):
+                multiply(accs[e], e, h, g)
 
         def close(e):
-            multiply(accs[e], e, 0, 2)
-            for g in range(PASSES):
-                multiply(accs[e], e, 1, g)
-            finish(accs[e], e, 0, C)
+            both(e, PASSES - 1)
+            nc.scalar.activation(y[:, e * C:(e + 1) * C], accs[e][:], GELU, bias=bias[:, e:e + 1])
 
-        accs = [psum.tile([P, C], F32, name="acc") for e in range(E)]
-        last = E - 1
+        accs = [psum.tile([P, C], F32, name=f"bank{e}") for e in range(E)]
         for e in range(E):
-            multiply(accs[e], e, 0, 0)
-        for e in range(E // 2):
-            multiply(accs[e], e, 0, 1)
-        for e in range(E // 2):
-            close(e)
-        for e in range(E // 2, E):
-            multiply(accs[e], e, 0, 1)
-        extra = psum.tile([P, C], F32, name="acc")
-        multiply(extra, last, 1, 0)
-        multiply(extra, last, 1, 1)
-        for e in range(E // 2, last):
-            close(e)
-        multiply(accs[last], last, 0, 2)
-        finish(accs[last], last, 0, P)
-        multiply(extra, last, 1, 2)
-        finish(extra, last, P, C)
+            both(e, 0)
+        for half in (range(E // 2), range(E // 2, E)):
+            for e in half:
+                both(e, 1)
+            for e in half:
+                close(e)
 
         parts = list(zip(TOKEN_CUTS, TOKEN_CUTS[1:]))
         lists = (pos1_sb, pos2_sb)
@@ -202,31 +190,26 @@ def tile_moe_cap2_lin_gelu_kernel(tc, xT, w_words, w_scales, b, gate, offs, pos1
             nc.vector.tensor_tensor(res[:], picked[i][0][:], picked[i][1][:], ADD)
             nc.sync.dma_start(out[:, a:z], res[:])
 
-        turned_sums = {}
-
-        def add_turned(i):
+        def add_on_tensor(i, steps):
             a, z = parts[i]
-            turned_sums[i] = psum.tile([P, z - a], F32, name="acc")
-            for c in range(0, z - a, P):
-                for r in range(2):
-                    nc.tensor.matmul(turned_sums[i][:, c:c + P], lhsT=picked[i][r][:, c:c + P], rhs=ident[:], is_transpose=True, start=(r == 0), stop=(r == 1))
-
-        def turn_back(i, tag):
-            a, z = parts[i]
-            summed = keep.tile([P, z - a], F32, name=tag, align_bytes=256)
-            nc.scalar.copy(summed[:], turned_sums[i][:])
-            back = psum.tile([P, z - a], F32, name="acc")
-            for c in range(0, z - a, P):
-                nc.tensor.transpose(back[:, c:c + P], summed[:, c:c + P], ident[:])
             res = keep.tile([P, z - a], F32, name=f"res{i}", align_bytes=256)
-            nc.scalar.copy(res[:], back[:])
+            for lo, hi, bank in steps:
+                turned_sum = psum.tile([P, hi - lo], F32, name=f"bank{bank}")
+                for c in range(lo, hi, P):
+                    for r in range(2):
+                        nc.tensor.matmul(turned_sum[:, c - lo:c - lo + P], lhsT=picked[i][r][:, c:c + P], rhs=ident[:], is_transpose=True, start=(r == 0), stop=(r == 1))
+                summed = keep.tile([P, hi - lo], F32, name=f"summed{bank}", align_bytes=256)
+                nc.scalar.copy(summed[:], turned_sum[:])
+                back = psum.tile([P, hi - lo], F32, name=f"bank{bank + 3}")
+                for c in range(0, hi - lo, P):
+                    nc.tensor.transpose(back[:, c:c + P], summed[:, c:c + P], ident[:])
+                nc.scalar.copy(res[:, lo:hi], back[:])
             nc.sync.dma_start(out[:, a:z], res[:])
 
-        for i in range(2):
+        for i, steps in enumerate((((0, 256, 0),), ((0, 128, 1), (128, 256, 2)))):
             pick(i, 0)
             pick(i, 1)
-            add_turned(i)
-            turn_back(i, f"summed{i}")
+            add_on_tensor(i, steps)
         pick(2, 0)
         pick(2, 1)
         pick(3, 0)

@@ -101,7 +101,10 @@ def tile_moe_cap2_lin_gelu_kernel(tc, xT, w_words, w_scales, b, gate, offs, pos1
                 for width, v in block:
                     src = raw[g][t0][:]
                     dst = mixed[:, t0 - first:t0 - first + width, :]
-                    if v < width:
+                    if (g, t0) == (1, 256):
+                        nc.gpsimd.tensor_copy(dst[:, :P, :].rearrange("p (c i) j -> p c j i", i=2), src[:, :, :P].rearrange("p j (c i) -> p c j i", i=2))
+                        nc.scalar.activation(dst[:, P:, :].rearrange("p (c i) j -> p c j i", i=2), src[:, :, P:].rearrange("p j (c i) -> p c j i", i=2), COPY)
+                    elif v < width:
                         nc.scalar.activation(
                             dst[:, v:, :].rearrange("p (c i) j -> p c j i", i=2), src[:, :, v:].rearrange("p j (c i) -> p c j i", i=2), COPY
                         )
@@ -146,7 +149,7 @@ def tile_moe_cap2_lin_gelu_kernel(tc, xT, w_words, w_scales, b, gate, offs, pos1
         for a, z in zip(LAST_CUTS, LAST_CUTS[1:]):
             gather_words(PASSES - 1, a, z)
 
-        def multiply(acc, e, h, g):
+        def multiply(acc, e, h, g, alone=False):
             s0 = e * C + h * P
             codes = held[:, h * P:(h + 1) * P] if e == E - 1 and g == 1 else slot_words[g][:, s0:s0 + P]
             nc.tensor.matmul_mx(
@@ -155,8 +158,8 @@ def tile_moe_cap2_lin_gelu_kernel(tc, xT, w_words, w_scales, b, gate, offs, pos1
                 lhsT_scale=ws_sb[:, e * PASSES + g, :],
                 rhs=codes.bitcast(FP8X4),
                 rhs_scale=moved[g][:, s0:s0 + P],
-                start=(g == 0 and h == 0),
-                stop=(g == PASSES - 1 and h == 1),
+                start=(g == 0 and (h == 0 or alone)),
+                stop=(g == PASSES - 1 and (h == 1 or alone)),
             )
 
         def both(e, g):
@@ -168,13 +171,26 @@ def tile_moe_cap2_lin_gelu_kernel(tc, xT, w_words, w_scales, b, gate, offs, pos1
             nc.scalar.activation(y[:, e * C:(e + 1) * C], accs[e][:], GELU, bias=bias[:, e:e + 1])
 
         accs = [psum.tile([P, C], F32, name=f"bank{e}") for e in range(E)]
-        for e in range(E):
+        last = E - 1
+        for e in range(last):
             both(e, 0)
-        for half in (range(E // 2), range(E // 2, E)):
-            for e in half:
-                both(e, 1)
-            for e in half:
-                close(e)
+        multiply(accs[last], last, 0, 0, True)
+        for e in range(E // 2):
+            both(e, 1)
+        for e in range(E // 2):
+            close(e)
+        extra = psum.tile([P, C], F32, name="bank0")
+        multiply(extra, last, 1, 0, True)
+        for e in range(E // 2, last):
+            both(e, 1)
+        halves = (accs[last], extra)
+        for h in range(2):
+            multiply(halves[h], last, h, 1, True)
+        for e in range(E // 2, last):
+            close(e)
+        for h in range(2):
+            multiply(halves[h], last, h, 2, True)
+            nc.scalar.activation(y[:, last * C + h * P:last * C + (h + 1) * P], halves[h][:, h * P:(h + 1) * P], GELU, bias=bias[:, last:last + 1])
 
         parts = list(zip(TOKEN_CUTS, TOKEN_CUTS[1:]))
         lists = (pos1_sb, pos2_sb)

@@ -143,8 +143,8 @@ def tile_moe_cap2_lin_gelu_kernel(tc, xT, w_words, w_scales, b, gate, offs, pos1
             nc.vector.tensor_copy(slot_planes[:, a:z], planes[:].indirect(offs_sb[:, a // 16:z // 16]))
             for g in (1, 2):
                 k = PLANE_ROW[g]
-                for r, rows in ((0, 64), (64, 4), (96, 4)):
-                    nc.sync.dma_start(moved[g][r:r + rows, a:z].bitcast(I32), slot_planes[r + k:r + k + rows, a:z].bitcast(I32))
+                for r in range(0, P, 32):
+                    nc.sync.dma_start(moved[g][r:r + 4, a:z].bitcast(I32), slot_planes[r + k:r + k + 4, a:z].bitcast(I32))
 
         for a, z in zip(LAST_CUTS, LAST_CUTS[1:]):
             gather_words(PASSES - 1, a, z)

@@ -26,7 +26,7 @@ GELU = mybir.ActivationFunctionType.Gelu_apprx_tanh
 
 BLOCKS = (
     (((256, 128),), ((256, 128),), ((256, 128),), ((256, 128),), ((128, 0),), ((128, 128),)),
-    (((128, 0), (128, 0), (256, 0)), ((256, 0), (256, 0)), ((128, 0),), ((128, 0),)),
+    (((256, 0), (256, 0)), ((256, 0), (256, 0)), ((128, 0),), ((128, 0),)),
     (((256, 0), (256, 0)), ((256, 0), (256, 0)), ((128, 0), (128, 0))),
 )
 PLANE_ROW = (0, 4, 8)
@@ -73,8 +73,7 @@ def tile_moe_cap2_lin_gelu_kernel(tc, xT, w_words, w_scales, b, gate, offs, pos1
                     t0 = t0 + width
             if g == 0:
                 nc.sync.dma_start(offs_sb[:], offs)
-                for a, z in ((0, 8), (8, 10)):
-                    nc.sync.dma_start(gate_rows[a:z, :, :], gate[:, 0, a * P:z * P].rearrange("r (c p) -> c r p", p=P))
+                nc.sync.dma_start(gate_rows[:T // P, :, :], gate[:, 0, :].rearrange("r (c p) -> c r p", p=P))
         nc.sync.dma_start(bias[:], b)
         nc.sync.dma_start(pos1_sb[:], pos1)
         nc.sync.dma_start(pos2_sb[:], pos2)
@@ -208,7 +207,7 @@ def tile_moe_cap2_lin_gelu_kernel(tc, xT, w_words, w_scales, b, gate, offs, pos1
 
         def add_on_tensor(i, steps):
             a, z = parts[i]
-            res = keep.tile([P, z - a], F32, name=f"res{i}", align_bytes=256)
+            res = first[:, a:z]
             for lo, hi, bank in steps:
                 turned_sum = psum.tile([P, hi - lo], F32, name=f"bank{bank}")
                 for c in range(lo, hi, P):
@@ -220,12 +219,13 @@ def tile_moe_cap2_lin_gelu_kernel(tc, xT, w_words, w_scales, b, gate, offs, pos1
                 for c in range(0, hi - lo, P):
                     nc.tensor.transpose(back[:, c:c + P], summed[:, c:c + P], ident[:])
                 nc.scalar.copy(res[:, lo:hi], back[:])
-            nc.sync.dma_start(out[:, a:z], res[:])
 
+        first = keep.tile([P, parts[1][1]], F32, name="first", align_bytes=256)
         for i, steps in enumerate((((0, 256, 0),), ((0, 128, 1), (128, 256, 2)))):
             pick(i, 0)
             pick(i, 1)
             add_on_tensor(i, steps)
+        nc.sync.dma_start(out[:, :parts[1][1]], first[:])
         pick(2, 0)
         pick(2, 1)
         pick(3, 0)

@@ -33,7 +33,7 @@ PLANE_ROW = (0, 4, 8)
 WIDE = 1376
 SLOT_CUTS = (0, 1024, 2048)
 LAST_CUTS = (0, 512, 1024, 1536, 1792, 2048)
-TOKEN_CUTS = (0, 256, 512, 896, 1152, 1280)
+TOKEN_CUTS = (0, 512, 896, 1152, 1280)
 
 
 def tile_moe_cap2_lin_gelu_kernel(tc, xT, w_words, w_scales, b, gate, offs, pos1, pos2, out):
@@ -193,17 +193,16 @@ def tile_moe_cap2_lin_gelu_kernel(tc, xT, w_words, w_scales, b, gate, offs, pos1
 
         parts = list(zip(TOKEN_CUTS, TOKEN_CUTS[1:]))
         lists = (pos1_sb, pos2_sb)
-        picked = [[keep.tile([P, z - a], F32, name=f"picked{r}_{a}", align_bytes=256) for r in range(2)] for a, z in parts]
+        picked = [[keep.tile([P, z - a], F32, name=f"picked{r}_{a}", align_bytes=256)[:] for r in range(2)] for a, z in parts[:-1]]
 
         def pick(i, r):
             a, z = parts[i]
-            nc.vector.tensor_tensor(picked[i][r][:], y[:].indirect(lists[r][:, a // 16:z // 16]), gates[:, r * T + a:r * T + z], MULT)
+            nc.vector.tensor_tensor(picked[i][r], y[:].indirect(lists[r][:, a // 16:z // 16]), gates[:, r * T + a:r * T + z], MULT)
 
-        def combine(i):
+        def combine(i, res):
             a, z = parts[i]
-            res = keep.tile([P, z - a], F32, name=f"res{i}", align_bytes=256)
-            nc.vector.tensor_tensor(res[:], picked[i][0][:], picked[i][1][:], ADD)
-            nc.sync.dma_start(out[:, a:z], res[:])
+            nc.vector.tensor_tensor(res, picked[i][0], picked[i][1], ADD)
+            nc.sync.dma_start(out[:, a:z], res)
 
         def add_on_tensor(i, steps):
             a, z = parts[i]
@@ -220,18 +219,21 @@ def tile_moe_cap2_lin_gelu_kernel(tc, xT, w_words, w_scales, b, gate, offs, pos1
                     nc.tensor.transpose(back[:, c:c + P], summed[:, c:c + P], ident[:])
                 nc.scalar.copy(res[:, lo:hi], back[:])
 
-        first = keep.tile([P, parts[1][1]], F32, name="first", align_bytes=256)
-        for i, steps in enumerate((((0, 256, 0),), ((0, 128, 1), (128, 256, 2)))):
+        first = keep.tile([P, parts[0][1]], F32, name="first", align_bytes=256)
+        for i, steps in enumerate((((0, 256, 0), (256, 384, 1), (384, 512, 2)),)):
             pick(i, 0)
             pick(i, 1)
             add_on_tensor(i, steps)
-        nc.sync.dma_start(out[:, :parts[1][1]], first[:])
+        nc.sync.dma_start(out[:, :parts[0][1]], first[:])
+        late = keep.tile([P, 4 * P], F32, name="summed2", align_bytes=256)
+        picked.append([late[:, :P], late[:, P:2 * P]])
+        res = keep.tile([P, 4 * P], F32, name="res", align_bytes=256)
+        pick(1, 0)
+        pick(1, 1)
         pick(2, 0)
+        combine(1, res[:, :3 * P])
         pick(2, 1)
         pick(3, 0)
-        combine(2)
         pick(3, 1)
-        pick(4, 0)
-        pick(4, 1)
-        combine(3)
-        combine(4)
+        combine(2, late[:, 2 * P:])
+        combine(3, res[:, 3 * P:])

@@ -27,7 +27,7 @@ GELU = mybir.ActivationFunctionType.Gelu_apprx_tanh
 BLOCKS = (
     (((256, 128),), ((256, 128),), ((256, 128),), ((256, 128),), ((128, 0),), ((128, 128),)),
     (((256, 0), (256, 0)), ((256, 0), (256, 0)), ((128, 0),), ((128, 0),)),
-    (((256, 0), (256, 0)), ((256, 0), (256, 0)), ((128, 0), (128, 0))),
+    (((256, 0), (256, 0)), ((256, 0), (256, 0)), ((256, 0),)),
 )
 PLANE_ROW = (0, 4, 8)
 WIDE = 1376
@@ -79,7 +79,8 @@ def tile_moe_cap2_lin_gelu_kernel(tc, xT, w_words, w_scales, b, gate, offs, pos1
         nc.sync.dma_start(pos2_sb[:], pos2)
         for q in range(4):
             nc.sync.dma_start(ws_sb[32 * q:32 * q + 4, :, :].bitcast(I32), w_scales[:, :, 4 * q:4 * q + 4, :].rearrange("e a q n -> q (e a) n").bitcast(I32))
-        nc.sync.dma_start(w_sb[:].rearrange("p g n -> p g n").bitcast(I32), w_words.rearrange("e a p n -> p (e a) n").bitcast(I32))
+        for e in (0, E // 2):
+            nc.sync.dma_start(w_sb[:, e * PASSES:(e + E // 2) * PASSES, :].bitcast(I32), w_words[e:e + E // 2].rearrange("e a p n -> p (e a) n").bitcast(I32))
 
         words = [keep.tile([P, WIDE if g < PASSES - 1 else T], U32, name=f"words{g}", align_bytes=256) for g in range(PASSES)]
         for g in range(PASSES - 1):
@@ -128,7 +129,7 @@ def tile_moe_cap2_lin_gelu_kernel(tc, xT, w_words, w_scales, b, gate, offs, pos1
                     c = col % 4
                     nc.tensor.transpose(spreads[col // 4][:, c * P:(c + 1) * P], gate_cols[:, col:col + 1].to_broadcast([P, P]), ident[:])
             if g == 2:
-                held = keep.tile([P, C], U32, name=f"raw{g}_{T - P}", align_bytes=256)
+                held = keep.tile([P, C], U32, name=f"raw{g}_{T - 2 * P}", align_bytes=256)
                 nc.vector.tensor_copy(held[:], words[1][:].indirect(offs_sb[:, (S - C) // 16:]))
             if g < PASSES - 1:
                 for a, z in ((0, 1024), (1024, S - g * C)):

@@ -33,7 +33,9 @@ PLANE_ROW = (0, 4, 8)
 WIDE = 1376
 SLOT_CUTS = (0, 1024, 2048)
 LAST_CUTS = (0, 512, 1024, 1536, 1792, 2048)
-TOKEN_CUTS = (0, 512, 896, 1152, 1280)
+FUSED = 640
+SECOND_CUTS = (0, 384, FUSED)
+BOTH_CUTS = (FUSED, 896, 1152, T)
 
 
 def tile_moe_cap2_lin_gelu_kernel(tc, xT, w_words, w_scales, b, gate, offs, pos1, pos2, out):
@@ -149,92 +151,74 @@ def tile_moe_cap2_lin_gelu_kernel(tc, xT, w_words, w_scales, b, gate, offs, pos1
         for a, z in zip(LAST_CUTS, LAST_CUTS[1:]):
             gather_words(PASSES - 1, a, z)
 
-        def multiply(acc, e, h, g, alone=False):
-            s0 = e * C + h * P
-            codes = held[:, h * P:(h + 1) * P] if e == E - 1 and g == 1 else slot_words[g][:, s0:s0 + P]
+        def multiply(acc, e, lo, hi, g):
+            s0 = e * C
+            codes = held[:, lo:hi] if e == E - 1 and g == 1 else slot_words[g][:, s0 + lo:s0 + hi]
             nc.tensor.matmul_mx(
-                out=acc[:, h * P:(h + 1) * P],
+                out=acc[:, lo:hi],
                 lhsT=w_sb[:, e * PASSES + g, :].bitcast(FP4X4),
                 lhsT_scale=ws_sb[:, e * PASSES + g, :],
                 rhs=codes.bitcast(FP8X4),
-                rhs_scale=moved[g][:, s0:s0 + P],
-                start=(g == 0 and (h == 0 or alone)),
-                stop=(g == PASSES - 1 and (h == 1 or alone)),
+                rhs_scale=moved[g][:, s0 + lo:s0 + hi],
+                start=(g == 0),
+                stop=(g == PASSES - 1),
             )
 
-        def both(e, g):
-            for h in range(2):
-                multiply(accs[e], e, h, g)
-
-        def close(e):
-            both(e, PASSES - 1)
-            nc.scalar.activation(y[:, e * C:(e + 1) * C], accs[e][:], GELU, bias=bias[:, e:e + 1])
+        def close(acc, e, lo, hi):
+            multiply(acc, e, lo, hi, PASSES - 1)
+            nc.scalar.activation(y[:, e * C + lo:e * C + hi], acc[:, lo:hi], GELU, bias=bias[:, e:e + 1])
 
         accs = [psum.tile([P, C], F32, name=f"bank{e}") for e in range(E)]
         last = E - 1
         for e in range(last):
-            both(e, 0)
-        multiply(accs[last], last, 0, 0, True)
+            multiply(accs[e], e, 0, C, 0)
+        multiply(accs[last], last, 0, P, 0)
         for e in range(E // 2):
-            both(e, 1)
+            multiply(accs[e], e, 0, C, 1)
         for e in range(E // 2):
-            close(e)
+            close(accs[e], e, 0, C)
         extra = psum.tile([P, C], F32, name="bank0")
-        multiply(extra, last, 1, 0, True)
+        multiply(extra, last, P, C, 0)
         for e in range(E // 2, last):
-            both(e, 1)
-        halves = (accs[last], extra)
-        for h in range(2):
-            multiply(halves[h], last, h, 1, True)
+            multiply(accs[e], e, 0, C, 1)
+        halves = ((accs[last], 0, P), (extra, P, C))
+        for acc, lo, hi in halves:
+            multiply(acc, last, lo, hi, 1)
         for e in range(E // 2, last):
-            close(e)
-        for h in range(2):
-            multiply(halves[h], last, h, 2, True)
-            nc.scalar.activation(y[:, last * C + h * P:last * C + (h + 1) * P], halves[h][:, h * P:(h + 1) * P], GELU, bias=bias[:, last:last + 1])
+            close(accs[e], e, 0, C)
+        for acc, lo, hi in halves:
+            close(acc, last, lo, hi)
 
-        parts = list(zip(TOKEN_CUTS, TOKEN_CUTS[1:]))
         lists = (pos1_sb, pos2_sb)
-        picked = [[keep.tile([P, z - a], F32, name=f"picked{r}_{a}", align_bytes=256)[:] for r in range(2)] for a, z in parts[:-1]]
+        gate_of = gates[:].rearrange("p (r t) -> p r t", r=2)
 
-        def pick(i, r):
-            a, z = parts[i]
-            nc.vector.tensor_tensor(picked[i][r], y[:].indirect(lists[r][:, a // 16:z // 16]), gates[:, r * T + a:r * T + z], MULT)
+        def looked_up(r, a, z):
+            return y[:].indirect(lists[r][:, a // 16:z // 16])
 
-        def combine(i, res):
-            a, z = parts[i]
-            nc.vector.tensor_tensor(res, picked[i][0], picked[i][1], ADD)
-            nc.sync.dma_start(out[:, a:z], res)
+        first = keep.tile([P, FUSED], F32, name="first", align_bytes=256)
+        nc.vector.tensor_tensor(first[:], looked_up(0, 0, FUSED), gates[:, :FUSED], MULT)
+        second = keep.tile([P, FUSED], F32, name="second", align_bytes=256)
+        for a, z in zip(SECOND_CUTS, SECOND_CUTS[1:]):
+            plain = keep.tile([P, z - a], F32, name=f"plain{a}", align_bytes=256)
+            nc.scalar.activation(plain[:], looked_up(1, a, z), COPY)
+            nc.vector.tensor_tensor(second[:, a:z], plain[:], gate_of[:, 1, a:z], MULT)
+        res = keep.tile([P, FUSED], F32, name="res0", align_bytes=256)
+        waiting = (res[:], first[:], second[:], 0, FUSED)
 
-        def add_on_tensor(i, steps):
-            a, z = parts[i]
-            res = first[:, a:z]
-            for lo, hi, bank in steps:
-                turned_sum = psum.tile([P, hi - lo], F32, name=f"bank{bank}")
-                for c in range(lo, hi, P):
-                    for r in range(2):
-                        nc.tensor.matmul(turned_sum[:, c - lo:c - lo + P], lhsT=picked[i][r][:, c:c + P], rhs=ident[:], is_transpose=True, start=(r == 0), stop=(r == 1))
-                summed = keep.tile([P, hi - lo], F32, name=f"summed{bank}", align_bytes=256)
-                nc.scalar.copy(summed[:], turned_sum[:])
-                back = psum.tile([P, hi - lo], F32, name=f"bank{bank + 3}")
-                for c in range(0, hi - lo, P):
-                    nc.tensor.transpose(back[:, c:c + P], summed[:, c:c + P], ident[:])
-                nc.scalar.copy(res[:, lo:hi], back[:])
+        def add_and_store(total, one, other, a, z):
+            nc.vector.tensor_tensor(total, one, other, ADD)
+            nc.sync.dma_start(out[:, a:z], total)
 
-        first = keep.tile([P, parts[0][1]], F32, name="first", align_bytes=256)
-        for i, steps in enumerate((((0, 256, 0), (256, 384, 1), (384, 512, 2)),)):
-            pick(i, 0)
-            pick(i, 1)
-            add_on_tensor(i, steps)
-        nc.sync.dma_start(out[:, :parts[0][1]], first[:])
-        late = keep.tile([P, 4 * P], F32, name="summed2", align_bytes=256)
-        picked.append([late[:, :P], late[:, P:2 * P]])
-        res = keep.tile([P, 4 * P], F32, name="res", align_bytes=256)
-        pick(1, 0)
-        pick(1, 1)
-        pick(2, 0)
-        combine(1, res[:, :3 * P])
-        pick(2, 1)
-        pick(3, 0)
-        pick(3, 1)
-        combine(2, late[:, 2 * P:])
-        combine(3, res[:, 3 * P:])
+        for a, z in zip(BOTH_CUTS, BOTH_CUTS[1:]):
+            pair = keep.tile([P, 2, z - a], F32, name=f"pair{a}", align_bytes=256)
+            for r in range(2):
+                nc.scalar.activation(pair[:, r, :], looked_up(r, a, z), COPY)
+            if a == FUSED:
+                add_and_store(*waiting)
+            gated = keep.tile([P, 2, z - a], F32, name=f"gated{a}", align_bytes=256)
+            nc.vector.tensor_tensor(gated[:], pair[:], gate_of[:, :, a:z], MULT)
+            if a != FUSED:
+                add_and_store(*waiting)
+            res = keep.tile([P, z - a], F32, name=f"res{a}", align_bytes=256)
+            waiting = (res[:], gated[:, 0, :], gated[:, 1, :], a, z)
+        add_and_store(*waiting)

@@ -33,9 +33,9 @@ PLANE_ROW = (0, 4, 8)
 WIDE = 1376
 SLOT_CUTS = (0, 1024, 2048)
 LAST_CUTS = (0, 512, 1024, 1536, 1792, 2048)
-FUSED = 640
-SECOND_CUTS = (0, 384, FUSED)
-BOTH_CUTS = (FUSED, 896, 1152, T)
+FUSED = 896
+SECOND_CUTS = (0, 512, FUSED)
+BOTH_CUTS = (FUSED, 1152, T)
 
 
 def tile_moe_cap2_lin_gelu_kernel(tc, xT, w_words, w_scales, b, gate, offs, pos1, pos2, out):
@@ -197,28 +197,28 @@ def tile_moe_cap2_lin_gelu_kernel(tc, xT, w_words, w_scales, b, gate, offs, pos1
 
         first = keep.tile([P, FUSED], F32, name="first", align_bytes=256)
         nc.vector.tensor_tensor(first[:], looked_up(0, 0, FUSED), gates[:, :FUSED], MULT)
-        second = keep.tile([P, FUSED], F32, name="second", align_bytes=256)
+        sums = []
         for a, z in zip(SECOND_CUTS, SECOND_CUTS[1:]):
             plain = keep.tile([P, z - a], F32, name=f"plain{a}", align_bytes=256)
             nc.scalar.activation(plain[:], looked_up(1, a, z), COPY)
-            nc.vector.tensor_tensor(second[:, a:z], plain[:], gate_of[:, 1, a:z], MULT)
-        res = keep.tile([P, FUSED], F32, name="res0", align_bytes=256)
-        waiting = (res[:], first[:], second[:], 0, FUSED)
+            second = keep.tile([P, z - a], F32, name=f"second{a}", align_bytes=256)
+            nc.vector.tensor_tensor(second[:], plain[:], gate_of[:, 1, a:z], MULT)
+            sums.append((first[:, a:z], second[:], a, z))
 
-        def add_and_store(total, one, other, a, z):
-            nc.vector.tensor_tensor(total, one, other, ADD)
-            nc.sync.dma_start(out[:, a:z], total)
+        def add_and_store(one, other, a, z):
+            total = keep.tile([P, z - a], F32, name=f"total{a}", align_bytes=256)
+            nc.vector.tensor_tensor(total[:], one, other, ADD)
+            nc.sync.dma_start(out[:, a:z], total[:])
 
+        for part in sums:
+            add_and_store(*part)
+        sums = []
         for a, z in zip(BOTH_CUTS, BOTH_CUTS[1:]):
             pair = keep.tile([P, 2, z - a], F32, name=f"pair{a}", align_bytes=256)
             for r in range(2):
                 nc.scalar.activation(pair[:, r, :], looked_up(r, a, z), COPY)
-            if a == FUSED:
-                add_and_store(*waiting)
             gated = keep.tile([P, 2, z - a], F32, name=f"gated{a}", align_bytes=256)
             nc.vector.tensor_tensor(gated[:], pair[:], gate_of[:, :, a:z], MULT)
-            if a != FUSED:
-                add_and_store(*waiting)
-            res = keep.tile([P, z - a], F32, name=f"res{a}", align_bytes=256)
-            waiting = (res[:], gated[:, 0, :], gated[:, 1, :], a, z)
-        add_and_store(*waiting)
+            sums.append((gated[:, 0, :], gated[:, 1, :], a, z))
+        for part in sums:
+            add_and_store(*part)

@@ -25,14 +25,14 @@ COPY = mybir.ActivationFunctionType.Copy
 GELU = mybir.ActivationFunctionType.Gelu_apprx_tanh
 
 BLOCKS = (
-    (((256, 128),), ((256, 128),), ((256, 128),), ((256, 128),), ((128, 0),), ((128, 128),)),
-    (((256, 0), (256, 0)), ((256, 0), (256, 0)), ((128, 0),), ((128, 0),)),
-    (((256, 0), (256, 0)), ((256, 0), (256, 0)), ((256, 0),)),
+    (((256, 128, 0),), ((256, 128, 0),), ((256, 128, 0),), ((256, 128, 0),), ((128, 0, 0),), ((128, 32, 0),)),
+    (((256, 0, 0), (256, 0, 128)), ((256, 0, 0), (256, 0, 0)), ((128, 0, 0),), ((128, 0, 0),)),
+    (((256, 0, 0), (256, 0, 0)), ((256, 0, 0), (256, 0, 0)), ((256, 0, 0),)),
 )
 PLANE_ROW = (0, 4, 8)
 WIDE = 1376
 SLOT_CUTS = (0, 1024, 2048)
-LAST_CUTS = (0, 512, 1024, 1536, 1792, 2048)
+LAST_CUTS = (0, 512, 1024, 1536, 1792, 1920, 2048)
 FUSED = 896
 SECOND_CUTS = (0, 512, FUSED)
 BOTH_CUTS = (FUSED, 1152, T)
@@ -68,7 +68,7 @@ def tile_moe_cap2_lin_gelu_kernel(tc, xT, w_words, w_scales, b, gate, offs, pos1
             raw.append({})
             t0 = 0
             for block in BLOCKS[g]:
-                for width, v in block:
+                for width, v, gp in block:
                     piece = keep.tile([P, PACK, width], F32, name=f"raw{g}_{t0}", align_bytes=256)
                     nc.sync.dma_start(piece[:], rows[:, :, t0:t0 + width])
                     raw[g][t0] = piece
@@ -98,17 +98,16 @@ def tile_moe_cap2_lin_gelu_kernel(tc, xT, w_words, w_scales, b, gate, offs, pos1
             k = PLANE_ROW[g]
             t0 = 0
             for block in BLOCKS[g]:
-                first, total = t0, sum(width for width, v in block)
+                first, total = t0, sum(width for width, v, gp in block)
                 mixed = keep.tile([P, total, PACK], BF16, name=f"mixed{g}_{t0}", align_bytes=256)
-                for width, v in block:
+                for width, v, gp in block:
                     src = raw[g][t0][:]
                     dst = mixed[:, t0 - first:t0 - first + width, :]
-                    if (g, t0) == (1, 256):
-                        nc.gpsimd.tensor_copy(dst[:, :P, :].rearrange("p (c i) j -> p c j i", i=2), src[:, :, :P].rearrange("p j (c i) -> p c j i", i=2))
-                        nc.scalar.activation(dst[:, P:, :].rearrange("p (c i) j -> p c j i", i=2), src[:, :, P:].rearrange("p j (c i) -> p c j i", i=2), COPY)
-                    elif v < width:
+                    if gp > 0:
+                        nc.gpsimd.tensor_copy(dst[:, v:v + gp, :].rearrange("p (c i) j -> p c j i", i=2), src[:, :, v:v + gp].rearrange("p j (c i) -> p c j i", i=2))
+                    if v + gp < width:
                         nc.scalar.activation(
-                            dst[:, v:, :].rearrange("p (c i) j -> p c j i", i=2), src[:, :, v:].rearrange("p j (c i) -> p c j i", i=2), COPY
+                            dst[:, v + gp:, :].rearrange("p (c i) j -> p c j i", i=2), src[:, :, v + gp:].rearrange("p j (c i) -> p c j i", i=2), COPY
                         )
                     if v > 0:
                         nc.vector.tensor_copy(
@@ -131,7 +130,7 @@ def tile_moe_cap2_lin_gelu_kernel(tc, xT, w_words, w_scales, b, gate, offs, pos1
                     c = col % 4
                     nc.tensor.transpose(spreads[col // 4][:, c * P:(c + 1) * P], gate_cols[:, col:col + 1].to_broadcast([P, P]), ident[:])
             if g == 2:
-                held = keep.tile([P, C], U32, name=f"raw{g}_{T - 2 * P}", align_bytes=256)
+                held = keep.tile([P, C], U32, name="raw2_1024", align_bytes=256)
                 nc.vector.tensor_copy(held[:], words[1][:].indirect(offs_sb[:, (S - C) // 16:]))
             if g < PASSES - 1:
                 for a, z in ((0, 1024), (1024, S - g * C)):

@@ -30,6 +30,7 @@ BLOCKS = (
     (((256, 0, 0), (256, 0, 0)), ((256, 0, 0), (256, 0, 0)), ((256, 0, 0),)),
 )
 PLANE_ROW = (0, 4, 8)
+QUADRANTS = (0, 2, 1, 3)
 WIDE = 1376
 SLOT_CUTS = (0, 1024, 2048)
 LAST_CUTS = (0, 512, 1024, 1536, 1792, 1920, 2048)
@@ -79,7 +80,7 @@ def tile_moe_cap2_lin_gelu_kernel(tc, xT, w_words, w_scales, b, gate, offs, pos1
         nc.sync.dma_start(bias[:], b)
         nc.sync.dma_start(pos1_sb[:], pos1)
         nc.sync.dma_start(pos2_sb[:], pos2)
-        for q in range(4):
+        for q in QUADRANTS:
             nc.sync.dma_start(ws_sb[32 * q:32 * q + 4, :, :].bitcast(I32), w_scales[:, :, 4 * q:4 * q + 4, :].rearrange("e a q n -> q (e a) n").bitcast(I32))
         for e in (0, E // 2):
             nc.sync.dma_start(w_sb[:, e * PASSES:(e + E // 2) * PASSES, :].bitcast(I32), w_words[e:e + E // 2].rearrange("e a p n -> p (e a) n").bitcast(I32))
@@ -144,7 +145,7 @@ def tile_moe_cap2_lin_gelu_kernel(tc, xT, w_words, w_scales, b, gate, offs, pos1
             nc.vector.tensor_copy(slot_planes[:, a:z], planes[:].indirect(offs_sb[:, a // 16:z // 16]))
             for g in (1, 2):
                 k = PLANE_ROW[g]
-                for r in range(0, P, 32):
+                for r in (32 * q for q in QUADRANTS):
                     nc.sync.dma_start(moved[g][r:r + 4, a:z].bitcast(I32), slot_planes[r + k:r + k + 4, a:z].bitcast(I32))
 
         for a, z in zip(LAST_CUTS, LAST_CUTS[1:]):

@@ -31,9 +31,11 @@ BLOCKS = (
 )
 PLANE_ROW = (0, 4, 8)
 QUADRANTS = (0, 2, 1, 3)
-WIDE = 1376
-SLOT_CUTS = (0, 1024, 2048)
-LAST_CUTS = (0, 512, 1024, 1536, 1792, 1920, 2048)
+LAST_WIDE = 1376
+PLANES_WIDE = 2048
+HELD = C
+BYTE_CUTS = (0, 1536, 2048)
+LAST_CUTS = (0, 1024, 1536, 1792, 1920, 2048)
 FUSED = 896
 SECOND_CUTS = (0, 512, FUSED)
 BOTH_CUTS = (FUSED, 1152, T)
@@ -45,22 +47,28 @@ def tile_moe_cap2_lin_gelu_kernel(tc, xT, w_words, w_scales, b, gate, offs, pos1
         keep = ctx.enter_context(tc.tile_pool(name="keep", bufs=1))
         psum = ctx.enter_context(tc.psum_pool(name="psum", bufs=1))
 
-        offs_sb = keep.tile([P, S // 16], U16, name="offs_sb", align_bytes=256)
-        pos1_sb = keep.tile([P, T // 16], U16, name="pos1_sb", align_bytes=256)
-        pos2_sb = keep.tile([P, T // 16], U16, name="pos2_sb", align_bytes=256)
-        bias = keep.tile([P, E], F32, name="bias", align_bytes=256)
-        planes = keep.tile([P, WIDE], U8, name="planes", align_bytes=256)
-        w_sb = keep.tile([P, E * PASSES, 2 * N], U8, name="w_sb", align_bytes=256)
-        ws_sb = keep.tile([P, E * PASSES, N], U8, name="ws_sb", align_bytes=256)
-        y = keep.tile([P, S + PAD], F32, name="y", align_bytes=256)
-        gate_rows = keep.tile([P, 2, P], F32, name="gate_rows", align_bytes=256)
-        ident = keep.tile([P, P], F32, name="ident", align_bytes=256)
-        zeros = keep.tile([P, PAD], F32, name="zeros", align_bytes=256)
+        def tile(shape, dtype, name):
+            return keep.tile(shape, dtype, name=name, align_bytes=256)
+
+        offs_sb = tile([P, S // 16], U16, "offs_sb")
+        pos1_sb = tile([P, T // 16], U16, "pos1_sb")
+        pos2_sb = tile([P, T // 16], U16, "pos2_sb")
+        bias = tile([P, E], F32, "bias")
+        planes = tile([P, PLANES_WIDE], U8, "planes")
+        w_sb = tile([P, E * PASSES, 2 * N], U8, "w_sb")
+        ws_sb = tile([P, E * PASSES, N], U8, "ws_sb")
+        y = tile([P, S + PAD], F32, "y")
+        gate_rows = tile([P, 2, P], F32, "gate_rows")
+        ident = tile([P, P], F32, "ident")
+        zeros = tile([P, PAD], F32, "zeros")
+        early_words = tile([P, T + 2 * S], U32, "early_words")
+        last_words = tile([P, LAST_WIDE], U32, "last_words")
+        words = (early_words[:, T:2 * T], early_words[:, :T], last_words[:, :T])
 
         nc.gpsimd.memset(zeros[:], 0.0)
         nc.scalar.activation(y[:, S:], zeros[:], GELU)
         nc.vector.memset(gate_rows[:].rearrange("p r c -> p (r c)"), 0.0)
-        nc.vector.memset(planes[:].bitcast(I32), 0)
+        nc.vector.memset(planes[:, :T].bitcast(I32), 0)
         make_identity(nc, ident[:])
 
         raw = []
@@ -70,7 +78,7 @@ def tile_moe_cap2_lin_gelu_kernel(tc, xT, w_words, w_scales, b, gate, offs, pos1
             t0 = 0
             for block in BLOCKS[g]:
                 for width, v, gp in block:
-                    piece = keep.tile([P, PACK, width], F32, name=f"raw{g}_{t0}", align_bytes=256)
+                    piece = tile([P, PACK, width], F32, f"raw{g}_{t0}")
                     nc.sync.dma_start(piece[:], rows[:, :, t0:t0 + width])
                     raw[g][t0] = piece
                     t0 = t0 + width
@@ -85,22 +93,18 @@ def tile_moe_cap2_lin_gelu_kernel(tc, xT, w_words, w_scales, b, gate, offs, pos1
         for e in (0, E // 2):
             nc.sync.dma_start(w_sb[:, e * PASSES:(e + E // 2) * PASSES, :].bitcast(I32), w_words[e:e + E // 2].rearrange("e a p n -> p (e a) n").bitcast(I32))
 
-        words = [keep.tile([P, WIDE if g < PASSES - 1 else T], U32, name=f"words{g}", align_bytes=256) for g in range(PASSES)]
-        for g in range(PASSES - 1):
-            nc.vector.memset(words[g][:, T:].bitcast(I32), 0)
-        slot_words = [keep.tile([P, S], U32, name=f"slot_words{g}", align_bytes=256) for g in range(PASSES)]
-        slot_planes = keep.tile([P, S], U8, name="slot_planes", align_bytes=256)
-        moved = [slot_planes] + [keep.tile([P, S], U8, name=f"moved{g}", align_bytes=256) for g in range(1, PASSES)]
+        slot_words = [tile([P, S - (HELD if g == 1 else 0)], U32, f"slot_words{g}") for g in range(PASSES)]
+        slot_planes = tile([P, S], U8, "slot_planes")
+        moved = [slot_planes] + [tile([P, S], U8, f"moved{g}") for g in range(1, PASSES)]
 
-        def gather_words(g, a, z):
-            nc.vector.tensor_copy(slot_words[g][:, a:z], words[g][:].indirect(offs_sb[:, a // 16:z // 16]))
+        def by_slots(window, a, z):
+            return window.indirect(offs_sb[:, a // 16:z // 16])
 
-        for g in range(PASSES):
-            k = PLANE_ROW[g]
+        def round_and_quantise(g):
             t0 = 0
             for block in BLOCKS[g]:
                 first, total = t0, sum(width for width, v, gp in block)
-                mixed = keep.tile([P, total, PACK], BF16, name=f"mixed{g}_{t0}", align_bytes=256)
+                mixed = tile([P, total, PACK], BF16, f"mixed{g}_{t0}")
                 for width, v, gp in block:
                     src = raw[g][t0][:]
                     dst = mixed[:, t0 - first:t0 - first + width, :]
@@ -117,39 +121,42 @@ def tile_moe_cap2_lin_gelu_kernel(tc, xT, w_words, w_scales, b, gate, offs, pos1
                     t0 = t0 + width
                 nc.vector.quantize_mx(
                     out=words[g][:, first:first + total].bitcast(FP8X4),
-                    scales=planes[k:P, first:first + total],
+                    scales=planes[PLANE_ROW[g]:P, first:first + total],
                     in_=mixed[:].rearrange("p t j -> p (t j)"),
                 )
-            if g == 1:
-                turned = psum.tile([P, 2, P], F32, name="bank2")
-                for r in range(2):
-                    nc.tensor.transpose(turned[:, r, :], gate_rows[:, r, :], ident[:])
-                gate_cols = keep.tile([P, 2 * T // P], F32, name="raw1_1152", align_bytes=256)
-                nc.vector.tensor_copy(gate_cols[:].rearrange("p (r c) -> p r c", r=2), turned[:, :, :T // P])
-                spreads = [psum.tile([P, 512], F32, name=f"bank{3 + bank}") for bank in range(2 * T // 512)]
-                for col in range(2 * T // P):
-                    c = col % 4
-                    nc.tensor.transpose(spreads[col // 4][:, c * P:(c + 1) * P], gate_cols[:, col:col + 1].to_broadcast([P, P]), ident[:])
-            if g == 2:
-                held = keep.tile([P, C], U32, name="raw2_1024", align_bytes=256)
-                nc.vector.tensor_copy(held[:], words[1][:].indirect(offs_sb[:, (S - C) // 16:]))
-            if g < PASSES - 1:
-                for a, z in ((0, 1024), (1024, S - g * C)):
-                    gather_words(g, a, z)
 
-        gates = keep.tile([P, 2 * T], F32, name="mixed2_1024", align_bytes=256)
+        round_and_quantise(0)
+        nc.vector.tensor_copy(slot_words[0][:], by_slots(early_words[:, T:], 0, S))
+
+        round_and_quantise(1)
+        turned = psum.tile([P, 2, P], F32, name="bank2")
+        for r in range(2):
+            nc.tensor.transpose(turned[:, r, :], gate_rows[:, r, :], ident[:])
+        gate_cols = tile([P, 2 * T // P], F32, "raw1_1152")
+        nc.vector.tensor_copy(gate_cols[:].rearrange("p (r c) -> p r c", r=2), turned[:, :, :T // P])
+        spreads = [psum.tile([P, 512], F32, name=f"bank{3 + bank}") for bank in range(2 * T // 512)]
+        for col in range(2 * T // P):
+            c = col % 4
+            nc.tensor.transpose(spreads[col // 4][:, c * P:(c + 1) * P], gate_cols[:, col:col + 1].to_broadcast([P, P]), ident[:])
+        nc.vector.tensor_copy(slot_words[1][:], by_slots(early_words[:, :2 * (S - HELD)], 0, S - HELD))
+
+        round_and_quantise(2)
+        held = tile([P, HELD], U32, "raw2_1024")
+        nc.vector.tensor_copy(held[:], by_slots(words[1], S - HELD, S))
+
+        gates = tile([P, 2 * T], F32, "mixed2_1024")
         for bank, spread in enumerate(spreads):
             nc.scalar.copy(gates[:, 512 * bank:512 * (bank + 1)], spread[:])
 
-        for a, z in zip(SLOT_CUTS, SLOT_CUTS[1:]):
-            nc.vector.tensor_copy(slot_planes[:, a:z], planes[:].indirect(offs_sb[:, a // 16:z // 16]))
+        for a, z in zip(BYTE_CUTS, BYTE_CUTS[1:]):
+            nc.vector.tensor_copy(slot_planes[:, a:z], by_slots(planes[:], a, z))
             for g in (1, 2):
                 k = PLANE_ROW[g]
                 for r in (32 * q for q in QUADRANTS):
                     nc.sync.dma_start(moved[g][r:r + 4, a:z].bitcast(I32), slot_planes[r + k:r + k + 4, a:z].bitcast(I32))
 
         for a, z in zip(LAST_CUTS, LAST_CUTS[1:]):
-            gather_words(PASSES - 1, a, z)
+            nc.vector.tensor_copy(slot_words[2][:, a:z], by_slots(last_words[:], a, z))
 
         def multiply(acc, e, lo, hi, g):
             s0 = e * C
@@ -170,16 +177,17 @@ def tile_moe_cap2_lin_gelu_kernel(tc, xT, w_words, w_scales, b, gate, offs, pos1
 
         accs = [psum.tile([P, C], F32, name=f"bank{e}") for e in range(E)]
         last = E - 1
+        ahead = BYTE_CUTS[1] // C
         for e in range(last):
             multiply(accs[e], e, 0, C, 0)
         multiply(accs[last], last, 0, P, 0)
-        for e in range(E // 2):
+        for e in range(ahead):
             multiply(accs[e], e, 0, C, 1)
         for e in range(E // 2):
             close(accs[e], e, 0, C)
         extra = psum.tile([P, C], F32, name="bank0")
         multiply(extra, last, P, C, 0)
-        for e in range(E // 2, last):
+        for e in range(ahead, last):
             multiply(accs[e], e, 0, C, 1)
         halves = ((accs[last], 0, P), (extra, P, C))
         for acc, lo, hi in halves:
@@ -195,18 +203,18 @@ def tile_moe_cap2_lin_gelu_kernel(tc, xT, w_words, w_scales, b, gate, offs, pos1
         def looked_up(r, a, z):
             return y[:].indirect(lists[r][:, a // 16:z // 16])
 
-        first = keep.tile([P, FUSED], F32, name="first", align_bytes=256)
+        first = tile([P, FUSED], F32, "first")
         nc.vector.tensor_tensor(first[:], looked_up(0, 0, FUSED), gates[:, :FUSED], MULT)
         sums = []
         for a, z in zip(SECOND_CUTS, SECOND_CUTS[1:]):
-            plain = keep.tile([P, z - a], F32, name=f"plain{a}", align_bytes=256)
+            plain = tile([P, z - a], F32, f"plain{a}")
             nc.scalar.activation(plain[:], looked_up(1, a, z), COPY)
-            second = keep.tile([P, z - a], F32, name=f"second{a}", align_bytes=256)
+            second = tile([P, z - a], F32, f"second{a}")
             nc.vector.tensor_tensor(second[:], plain[:], gate_of[:, 1, a:z], MULT)
             sums.append((first[:, a:z], second[:], a, z))
 
         def add_and_store(one, other, a, z):
-            total = keep.tile([P, z - a], F32, name=f"total{a}", align_bytes=256)
+            total = tile([P, z - a], F32, f"total{a}")
             nc.vector.tensor_tensor(total[:], one, other, ADD)
             nc.sync.dma_start(out[:, a:z], total[:])
 
@@ -214,10 +222,10 @@ def tile_moe_cap2_lin_gelu_kernel(tc, xT, w_words, w_scales, b, gate, offs, pos1
             add_and_store(*part)
         sums = []
         for a, z in zip(BOTH_CUTS, BOTH_CUTS[1:]):
-            pair = keep.tile([P, 2, z - a], F32, name=f"pair{a}", align_bytes=256)
+            pair = tile([P, 2, z - a], F32, f"pair{a}")
             for r in range(2):
                 nc.scalar.activation(pair[:, r, :], looked_up(r, a, z), COPY)
-            gated = keep.tile([P, 2, z - a], F32, name=f"gated{a}", align_bytes=256)
+            gated = tile([P, 2, z - a], F32, f"gated{a}")
             nc.vector.tensor_tensor(gated[:], pair[:], gate_of[:, :, a:z], MULT)
             sums.append((gated[:, 0, :], gated[:, 1, :], a, z))
         for part in sums:

@@ -32,10 +32,10 @@ BLOCKS = (
 PLANE_ROW = (0, 4, 8)
 QUADRANTS = (0, 2, 1, 3)
 LAST_WIDE = 1376
-PLANES_WIDE = 2048
+PLANES_WIDE = 1376
 HELD = C
-BYTE_CUTS = (0, 1536, 2048)
-LAST_CUTS = (0, 1024, 1536, 1792, 1920, 2048)
+BYTE_CUTS = (0, 1024, 2048)
+LAST_CUTS = (0, 512, 1024, 1536, 1792, 1920, 2048)
 FUSED = 896
 SECOND_CUTS = (0, 512, FUSED)
 BOTH_CUTS = (FUSED, 1152, T)

@@ -32,10 +32,10 @@ BLOCKS = (
 PLANE_ROW = (0, 4, 8)
 QUADRANTS = (0, 2, 1, 3)
 LAST_WIDE = 1376
-PLANES_WIDE = 1376
+PLANES_WIDE = 1728
 HELD = C
-BYTE_CUTS = (0, 1024, 2048)
-LAST_CUTS = (0, 512, 1024, 1536, 1792, 1920, 2048)
+BYTE_CUTS = (0, 1280, 2048)
+LAST_CUTS = (0, 768, 1280, 1536, 1792, 1920, 2048)
 FUSED = 896
 SECOND_CUTS = (0, 512, FUSED)
 BOTH_CUTS = (FUSED, 1152, T)
@@ -183,16 +183,19 @@ def tile_moe_cap2_lin_gelu_kernel(tc, xT, w_words, w_scales, b, gate, offs, pos1
         multiply(accs[last], last, 0, P, 0)
         for e in range(ahead):
             multiply(accs[e], e, 0, C, 1)
-        for e in range(E // 2):
+        early = LAST_CUTS[1] // C
+        for e in range(early):
             close(accs[e], e, 0, C)
         extra = psum.tile([P, C], F32, name="bank0")
         multiply(extra, last, P, C, 0)
+        for e in range(early, ahead):
+            close(accs[e], e, 0, C)
         for e in range(ahead, last):
             multiply(accs[e], e, 0, C, 1)
         halves = ((accs[last], 0, P), (extra, P, C))
         for acc, lo, hi in halves:
             multiply(acc, last, lo, hi, 1)
-        for e in range(E // 2, last):
+        for e in range(ahead, last):
             close(accs[e], e, 0, C)
         for acc, lo, hi in halves:
             close(acc, last, lo, hi)

@@ -24,10 +24,21 @@ ADD = mybir.AluOpType.add
 COPY = mybir.ActivationFunctionType.Copy
 GELU = mybir.ActivationFunctionType.Gelu_apprx_tanh
 
+LOADS = (
+    (256, 256, 256, 256, 128, 128),
+    (384, 256, 256, 128, 128, 128),
+    (384, 256, 256, 128, 128, 128),
+)
+V, G, A = "vector", "gpsimd", "scalar"
+PIECES = (
+    4 * ((V, 128), (A, 128)) + ((V, 64), (A, 64), (A, 64), (V, 64)),
+    ((G, 112), (A, 272), (A, 256), (G, 48), (A, 208), (A, 128), (A, 128), (A, 128)),
+    ((G, 112), (A, 272), (A, 256), (G, 48), (A, 208), (A, 128), (A, 128), (A, 128)),
+)
 BLOCKS = (
-    (((256, 128, 0),), ((256, 128, 0),), ((256, 128, 0),), ((256, 128, 0),), ((128, 0, 0),), ((128, 32, 0),)),
-    (((256, 0, 0), (256, 0, 128)), ((256, 0, 0), (256, 0, 0)), ((128, 0, 0),), ((128, 0, 0),)),
-    (((256, 0, 0), (256, 0, 0)), ((256, 0, 0), (256, 0, 0)), ((256, 0, 0),)),
+    (256, 256, 256, 256, 128, 64, 64),
+    (512, 512, 128, 128),
+    (512, 512, 128, 128),
 )
 PLANE_ROW = (0, 4, 8)
 QUADRANTS = (0, 2, 1, 3)
@@ -74,14 +85,13 @@ def tile_moe_cap2_lin_gelu_kernel(tc, xT, w_words, w_scales, b, gate, offs, pos1
         raw = []
         for g in range(PASSES):
             rows = xT[g * P * PACK:(g + 1) * P * PACK, :].rearrange("(p j) t -> p j t", j=PACK)
-            raw.append({})
+            raw.append([])
             t0 = 0
-            for block in BLOCKS[g]:
-                for width, v, gp in block:
-                    piece = tile([P, PACK, width], F32, f"raw{g}_{t0}")
-                    nc.sync.dma_start(piece[:], rows[:, :, t0:t0 + width])
-                    raw[g][t0] = piece
-                    t0 = t0 + width
+            for width in LOADS[g]:
+                loaded = tile([P, PACK, width], F32, f"raw{g}_{t0}")
+                nc.sync.dma_start(loaded[:], rows[:, :, t0:t0 + width])
+                raw[g].append((t0, loaded))
+                t0 = t0 + width
             if g == 0:
                 nc.sync.dma_start(offs_sb[:], offs)
                 nc.sync.dma_start(gate_rows[:T // P, :, :], gate[:, 0, :].rearrange("r (c p) -> c r p", p=P))
@@ -101,29 +111,29 @@ def tile_moe_cap2_lin_gelu_kernel(tc, xT, w_words, w_scales, b, gate, offs, pos1
             return window.indirect(offs_sb[:, a // 16:z // 16])
 
         def round_and_quantise(g):
-            t0 = 0
-            for block in BLOCKS[g]:
-                first, total = t0, sum(width for width, v, gp in block)
-                mixed = tile([P, total, PACK], BF16, f"mixed{g}_{t0}")
-                for width, v, gp in block:
-                    src = raw[g][t0][:]
-                    dst = mixed[:, t0 - first:t0 - first + width, :]
-                    if gp > 0:
-                        nc.gpsimd.tensor_copy(dst[:, v:v + gp, :].rearrange("p (c i) j -> p c j i", i=2), src[:, :, v:v + gp].rearrange("p j (c i) -> p c j i", i=2))
-                    if v + gp < width:
-                        nc.scalar.activation(
-                            dst[:, v + gp:, :].rearrange("p (c i) j -> p c j i", i=2), src[:, :, v + gp:].rearrange("p j (c i) -> p c j i", i=2), COPY
-                        )
-                    if v > 0:
-                        nc.vector.tensor_copy(
-                            dst[:, :v, :].rearrange("p (c i) j -> p c j i", i=4), src[:, :, :v].rearrange("p j (c i) -> p c j i", i=4)
-                        )
-                    t0 = t0 + width
-                nc.vector.quantize_mx(
-                    out=words[g][:, first:first + total].bitcast(FP8X4),
-                    scales=planes[PLANE_ROW[g]:P, first:first + total],
-                    in_=mixed[:].rearrange("p t j -> p (t j)"),
-                )
+            mixed = tile([P, T, PACK], BF16, f"mixed{g}")
+            blocks = list(BLOCKS[g])
+            t0 = first = 0
+            for engine, width in PIECES[g]:
+                start, loaded = [load for load in raw[g] if load[0] <= t0][-1]
+                i = 4 if engine == V else 2
+                src = loaded[:, :, t0 - start:t0 - start + width].rearrange("p j (c i) -> p c j i", i=i)
+                dst = mixed[:, t0:t0 + width, :].rearrange("p (c i) j -> p c j i", i=i)
+                if engine == A:
+                    nc.scalar.activation(dst, src, COPY)
+                elif engine == V:
+                    nc.vector.tensor_copy(dst, src)
+                else:
+                    nc.gpsimd.tensor_copy(dst, src)
+                t0 = t0 + width
+                if blocks[0] <= t0 - first:
+                    last = first + blocks.pop(0)
+                    nc.vector.quantize_mx(
+                        out=words[g][:, first:last].bitcast(FP8X4),
+                        scales=planes[PLANE_ROW[g]:P, first:last],
+                        in_=mixed[:, first:last, :].rearrange("p t j -> p (t j)"),
+                    )
+                    first = last
 
         round_and_quantise(0)
         nc.vector.tensor_copy(slot_words[0][:], by_slots(early_words[:, T:], 0, S))
@@ -141,10 +151,10 @@ def tile_moe_cap2_lin_gelu_kernel(tc, xT, w_words, w_scales, b, gate, offs, pos1
         nc.vector.tensor_copy(slot_words[1][:], by_slots(early_words[:, :2 * (S - HELD)], 0, S - HELD))
 
         round_and_quantise(2)
-        held = tile([P, HELD], U32, "raw2_1024")
+        held = tile([P, HELD], U32, "raw2_1152")
         nc.vector.tensor_copy(held[:], by_slots(words[1], S - HELD, S))
 
-        gates = tile([P, 2 * T], F32, "mixed2_1024")
+        gates = tile([P, 2 * T], F32, "mixed2")
         for bank, spread in enumerate(spreads):
             nc.scalar.copy(gates[:, 512 * bank:512 * (bank + 1)], spread[:])
 
@@ -221,8 +231,10 @@ def tile_moe_cap2_lin_gelu_kernel(tc, xT, w_words, w_scales, b, gate, offs, pos1
             nc.vector.tensor_tensor(total[:], one, other, ADD)
             nc.sync.dma_start(out[:, a:z], total[:])
 
-        for part in sums:
-            add_and_store(*part)
+        mixed_total = tile([P, FUSED], F32, "mixed_total")
+        for one, other, a, z in sums:
+            nc.vector.tensor_tensor(mixed_total[:, a:z], one, other, ADD)
+        nc.sync.dma_start(out[:, :FUSED], mixed_total[:])
         sums = []
         for a, z in zip(BOTH_CUTS, BOTH_CUTS[1:]):
             pair = tile([P, 2, z - a], F32, f"pair{a}")

@@ -27,18 +27,18 @@ GELU = mybir.ActivationFunctionType.Gelu_apprx_tanh
 LOADS = (
     (256, 256, 256, 256, 128, 128),
     (384, 256, 256, 128, 128, 128),
-    (384, 256, 256, 128, 128, 128),
+    (256, 256, 256, 256, 256),
 )
 V, G, A = "vector", "gpsimd", "scalar"
 PIECES = (
     4 * ((V, 128), (A, 128)) + ((V, 64), (A, 64), (A, 64), (V, 64)),
     ((G, 112), (A, 272), (A, 256), (G, 48), (A, 208), (A, 128), (A, 128), (A, 128)),
-    ((G, 112), (A, 272), (A, 256), (G, 48), (A, 208), (A, 128), (A, 128), (A, 128)),
+    3 * ((G, 64), (A, 192)) + ((A, 256), (A, 256)),
 )
 BLOCKS = (
     (256, 256, 256, 256, 128, 64, 64),
     (512, 512, 128, 128),
-    (512, 512, 128, 128),
+    (512, 512, 256),
 )
 PLANE_ROW = (0, 4, 8)
 QUADRANTS = (0, 2, 1, 3)
@@ -48,7 +48,7 @@ HELD = C
 BYTE_CUTS = (0, 1280, 2048)
 LAST_CUTS = (0, 768, 1280, 1536, 1792, 1920, 2048)
 FUSED = 896
-SECOND_CUTS = (0, 512, FUSED)
+SECOND_CUTS = (0, 576, FUSED)
 BOTH_CUTS = (FUSED, 1152, T)
 
 
@@ -139,24 +139,34 @@ def tile_moe_cap2_lin_gelu_kernel(tc, xT, w_words, w_scales, b, gate, offs, pos1
         nc.vector.tensor_copy(slot_words[0][:], by_slots(early_words[:, T:], 0, S))
 
         round_and_quantise(1)
-        turned = psum.tile([P, 2, P], F32, name="bank2")
+        turned = psum.tile([P, 2, P], F32, name="bank0")
         for r in range(2):
             nc.tensor.transpose(turned[:, r, :], gate_rows[:, r, :], ident[:])
         gate_cols = tile([P, 2 * T // P], F32, "raw1_1152")
         nc.vector.tensor_copy(gate_cols[:].rearrange("p (r c) -> p r c", r=2), turned[:, :, :T // P])
-        spreads = [psum.tile([P, 512], F32, name=f"bank{3 + bank}") for bank in range(2 * T // 512)]
-        for col in range(2 * T // P):
-            c = col % 4
-            nc.tensor.transpose(spreads[col // 4][:, c * P:(c + 1) * P], gate_cols[:, col:col + 1].to_broadcast([P, P]), ident[:])
+        blocks, fused = T // P, FUSED // P
+        copied = [r * blocks + c for r in range(2) for c in range(fused)]
+        spreads = [psum.tile([P, 512], F32, name=f"bank{1 + bank}") for bank in range(4)]
+        for i, col in enumerate(copied):
+            nc.tensor.transpose(spreads[i // 4][:, i % 4 * P:(i % 4 + 1) * P], gate_cols[:, col:col + 1].to_broadcast([P, P]), ident[:])
+        pair_gates = []
+        for bank, (a, z) in enumerate(zip(BOTH_CUTS, BOTH_CUTS[1:])):
+            kept = psum.tile([P, 2, z - a], F32, name=f"bank{6 + bank}")
+            for r in range(2):
+                for c in range(a // P, z // P):
+                    col = r * blocks + c
+                    nc.tensor.transpose(kept[:, r, c * P - a:(c + 1) * P - a], gate_cols[:, col:col + 1].to_broadcast([P, P]), ident[:])
+            pair_gates.append(kept)
         nc.vector.tensor_copy(slot_words[1][:], by_slots(early_words[:, :2 * (S - HELD)], 0, S - HELD))
 
         round_and_quantise(2)
-        held = tile([P, HELD], U32, "raw2_1152")
+        held = tile([P, HELD], U32, "raw2_1024")
         nc.vector.tensor_copy(held[:], by_slots(words[1], S - HELD, S))
 
-        gates = tile([P, 2 * T], F32, "mixed2")
+        gates = tile([P, 2 * FUSED], F32, "mixed2")
         for bank, spread in enumerate(spreads):
-            nc.scalar.copy(gates[:, 512 * bank:512 * (bank + 1)], spread[:])
+            width = min(512, 2 * FUSED - 512 * bank)
+            nc.scalar.copy(gates[:, 512 * bank:512 * bank + width], spread[:, :width])
 
         for a, z in zip(BYTE_CUTS, BYTE_CUTS[1:]):
             nc.vector.tensor_copy(slot_planes[:, a:z], by_slots(planes[:], a, z))
@@ -168,7 +178,7 @@ def tile_moe_cap2_lin_gelu_kernel(tc, xT, w_words, w_scales, b, gate, offs, pos1
         for a, z in zip(LAST_CUTS, LAST_CUTS[1:]):
             nc.vector.tensor_copy(slot_words[2][:, a:z], by_slots(last_words[:], a, z))
 
-        def multiply(acc, e, lo, hi, g):
+        def multiply(acc, e, lo, hi, g, opens=True, closes=True):
             s0 = e * C
             codes = held[:, lo:hi] if e == E - 1 and g == 1 else slot_words[g][:, s0 + lo:s0 + hi]
             nc.tensor.matmul_mx(
@@ -177,38 +187,49 @@ def tile_moe_cap2_lin_gelu_kernel(tc, xT, w_words, w_scales, b, gate, offs, pos1
                 lhsT_scale=ws_sb[:, e * PASSES + g, :],
                 rhs=codes.bitcast(FP8X4),
                 rhs_scale=moved[g][:, s0 + lo:s0 + hi],
-                start=(g == 0),
-                stop=(g == PASSES - 1),
+                start=(g == 0 and opens),
+                stop=(g == PASSES - 1 and closes),
             )
 
-        def close(acc, e, lo, hi):
-            multiply(acc, e, lo, hi, PASSES - 1)
+        banks = [psum.tile([P, 2, C], F32, name=f"bank{i}") for i in range(6)]
+        place = {0: (banks[0][:, 0, :], True, False), 1: (banks[0][:, 1, :], False, True), 2: (banks[1][:, 0, :], True, True),
+                 3: (banks[2][:, 0, :], True, False), 4: (banks[2][:, 1, :], False, True), 5: (banks[3][:, 0, :], True, True),
+                 6: (banks[4][:, 0, :], True, True)}
+
+        def product(e, g):
+            multiply(place[e][0], e, 0, C, g, place[e][1], place[e][2])
+
+        def gelu(acc, e, lo, hi):
             nc.scalar.activation(y[:, e * C + lo:e * C + hi], acc[:, lo:hi], GELU, bias=bias[:, e:e + 1])
 
-        accs = [psum.tile([P, C], F32, name=f"bank{e}") for e in range(E)]
+        def close(experts):
+            for e in experts:
+                product(e, PASSES - 1)
+            for e in experts:
+                gelu(place[e][0], e, 0, C)
+
         last = E - 1
         ahead = BYTE_CUTS[1] // C
         for e in range(last):
-            multiply(accs[e], e, 0, C, 0)
-        multiply(accs[last], last, 0, P, 0)
+            product(e, 0)
+        multiply(banks[5][:, 0, :], last, 0, P, 0)
         for e in range(ahead):
-            multiply(accs[e], e, 0, C, 1)
-        early = LAST_CUTS[1] // C
-        for e in range(early):
-            close(accs[e], e, 0, C)
-        extra = psum.tile([P, C], F32, name="bank0")
-        multiply(extra, last, P, C, 0)
-        for e in range(early, ahead):
-            close(accs[e], e, 0, C)
+            product(e, 1)
+        close((0, 1))
+        close((2,))
+        extra = psum.tile([P, 2, C], F32, name="bank0")
+        multiply(extra[:, 0, :], last, P, C, 0)
+        close((3, 4))
         for e in range(ahead, last):
-            multiply(accs[e], e, 0, C, 1)
-        halves = ((accs[last], 0, P), (extra, P, C))
+            product(e, 1)
+        halves = ((banks[5][:, 0, :], 0, P), (extra[:, 0, :], P, C))
         for acc, lo, hi in halves:
             multiply(acc, last, lo, hi, 1)
         for e in range(ahead, last):
-            close(accs[e], e, 0, C)
+            close((e,))
         for acc, lo, hi in halves:
-            close(acc, last, lo, hi)
+            multiply(acc, last, lo, hi, PASSES - 1)
+            gelu(acc, last, lo, hi)
 
         lists = (pos1_sb, pos2_sb)
         gate_of = gates[:].rearrange("p (r t) -> p r t", r=2)
@@ -226,22 +247,20 @@ def tile_moe_cap2_lin_gelu_kernel(tc, xT, w_words, w_scales, b, gate, offs, pos1
             nc.vector.tensor_tensor(second[:], plain[:], gate_of[:, 1, a:z], MULT)
             sums.append((first[:, a:z], second[:], a, z))
 
-        def add_and_store(one, other, a, z):
+        def add_and_store(one, other, a, z, engine=nc.vector):
             total = tile([P, z - a], F32, f"total{a}")
-            nc.vector.tensor_tensor(total[:], one, other, ADD)
+            engine.tensor_tensor(total[:], one, other, ADD)
             nc.sync.dma_start(out[:, a:z], total[:])
 
-        mixed_total = tile([P, FUSED], F32, "mixed_total")
-        for one, other, a, z in sums:
-            nc.vector.tensor_tensor(mixed_total[:, a:z], one, other, ADD)
-        nc.sync.dma_start(out[:, :FUSED], mixed_total[:])
+        add_and_store(*sums[0])
+        add_and_store(*sums[1], nc.gpsimd)
         sums = []
-        for a, z in zip(BOTH_CUTS, BOTH_CUTS[1:]):
+        for kept, (a, z) in zip(pair_gates, zip(BOTH_CUTS, BOTH_CUTS[1:])):
             pair = tile([P, 2, z - a], F32, f"pair{a}")
             for r in range(2):
                 nc.scalar.activation(pair[:, r, :], looked_up(r, a, z), COPY)
             gated = tile([P, 2, z - a], F32, f"gated{a}")
-            nc.vector.tensor_tensor(gated[:], pair[:], gate_of[:, :, a:z], MULT)
+            nc.vector.tensor_tensor(gated[:], pair[:], kept[:], MULT)
             sums.append((gated[:, 0, :], gated[:, 1, :], a, z))
         for part in sums:
             add_and_store(*part)

from contextlib import ExitStack

import concourse.mybir as mybir
from concourse.masks import make_identity

K, T, E, C, N = 1536, 1280, 8, 256, 128
S = E * C
PAD = 32
P = 128
PACK = 4
PASSES = K // (P * PACK)
FLOPS = 2 * K * N * S

F32 = mybir.dt.float32
BF16 = mybir.dt.bfloat16
U32 = mybir.dt.uint32
I32 = mybir.dt.int32
U16 = mybir.dt.uint16
U8 = mybir.dt.uint8
FP8X4 = mybir.dt.float8_e4m3fn_x4
FP4X4 = mybir.dt.float4_e2m1fn_x4
MULT = mybir.AluOpType.mult
ADD = mybir.AluOpType.add
COPY = mybir.ActivationFunctionType.Copy
GELU = mybir.ActivationFunctionType.Gelu_apprx_tanh

LOADS = (
    (256, 256, 256, 256, 128, 128),
    (384, 256, 256, 128, 128, 128),
    (256, 256, 256, 256, 256),
)
V, G, A = "vector", "gpsimd", "scalar"
PIECES = (
    4 * ((V, 128), (A, 128)) + ((V, 64), (A, 64), (A, 64), (V, 64)),
    ((G, 112), (A, 272), (A, 256), (G, 48), (A, 208), (A, 128), (A, 128), (A, 128)),
    3 * ((G, 64), (A, 192)) + ((A, 256), (A, 256)),
)
BLOCKS = (
    (256, 256, 256, 256, 128, 64, 64),
    (512, 512, 128, 128),
    (512, 512, 256),
)
PLANE_ROW = (0, 4, 8)
QUADRANTS = (0, 2, 1, 3)
LAST_WIDE = 1376
PLANES_WIDE = 1728
HELD = C
BYTE_CUTS = (0, 1280, 2048)
LAST_CUTS = (0, 768, 1280, 1536, 1792, 1920, 2048)
FUSED = 896
SECOND_CUTS = (0, 576, FUSED)
BOTH_CUTS = (FUSED, 1152, T)


def tile_moe_cap2_lin_gelu_kernel(tc, xT, w_words, w_scales, b, gate, offs, pos1, pos2, out):
    nc = tc.nc
    with ExitStack() as ctx:
        keep = ctx.enter_context(tc.tile_pool(name="keep", bufs=1))
        psum = ctx.enter_context(tc.psum_pool(name="psum", bufs=1))

        def tile(shape, dtype, name):
            return keep.tile(shape, dtype, name=name, align_bytes=256)

        offs_sb = tile([P, S // 16], U16, "offs_sb")
        pos1_sb = tile([P, T // 16], U16, "pos1_sb")
        pos2_sb = tile([P, T // 16], U16, "pos2_sb")
        bias = tile([P, E], F32, "bias")
        planes = tile([P, PLANES_WIDE], U8, "planes")
        w_sb = tile([P, E * PASSES, 2 * N], U8, "w_sb")
        ws_sb = tile([P, E * PASSES, N], U8, "ws_sb")
        y = tile([P, S + PAD], F32, "y")
        gate_rows = tile([P, 2, P], F32, "gate_rows")
        ident = tile([P, P], F32, "ident")
        zeros = tile([P, PAD], F32, "zeros")
        early_words = tile([P, T + 2 * S], U32, "early_words")
        last_words = tile([P, LAST_WIDE], U32, "last_words")
        words = (early_words[:, T:2 * T], early_words[:, :T], last_words[:, :T])

        nc.gpsimd.memset(zeros[:], 0.0)
        nc.scalar.activation(y[:, S:], zeros[:], GELU)
        nc.vector.memset(gate_rows[:].rearrange("p r c -> p (r c)"), 0.0)
        nc.vector.memset(planes[:, :T].bitcast(I32), 0)
        make_identity(nc, ident[:])

        raw = []
        for g in range(PASSES):
            rows = xT[g * P * PACK:(g + 1) * P * PACK, :].rearrange("(p j) t -> p j t", j=PACK)
            raw.append([])
            t0 = 0
            for width in LOADS[g]:
                loaded = tile([P, PACK, width], F32, f"raw{g}_{t0}")
                nc.sync.dma_start(loaded[:], rows[:, :, t0:t0 + width])
                raw[g].append((t0, loaded))
                t0 = t0 + width
            if g == 0:
                nc.sync.dma_start(offs_sb[:], offs)
                nc.sync.dma_start(gate_rows[:T // P, :, :], gate[:, 0, :].rearrange("r (c p) -> c r p", p=P))
        nc.sync.dma_start(bias[:], b)
        nc.sync.dma_start(pos1_sb[:], pos1)
        nc.sync.dma_start(pos2_sb[:], pos2)
        for q in QUADRANTS:
            nc.sync.dma_start(ws_sb[32 * q:32 * q + 4, :, :].bitcast(I32), w_scales[:, :, 4 * q:4 * q + 4, :].rearrange("e a q n -> q (e a) n").bitcast(I32))
        for e in (0, E // 2):
            nc.sync.dma_start(w_sb[:, e * PASSES:(e + E // 2) * PASSES, :].bitcast(I32), w_words[e:e + E // 2].rearrange("e a p n -> p (e a) n").bitcast(I32))

        slot_words = [tile([P, S - (HELD if g == 1 else 0)], U32, f"slot_words{g}") for g in range(PASSES)]
        slot_planes = tile([P, S], U8, "slot_planes")
        moved = [slot_planes] + [tile([P, S], U8, f"moved{g}") for g in range(1, PASSES)]

        def by_slots(window, a, z):
            return window.indirect(offs_sb[:, a // 16:z // 16])

        def round_and_quantise(g):
            mixed = tile([P, T, PACK], BF16, f"mixed{g}")
            blocks = list(BLOCKS[g])
            t0 = first = 0
            for engine, width in PIECES[g]:
                start, loaded = [load for load in raw[g] if load[0] <= t0][-1]
                i = 4 if engine == V else 2
                src = loaded[:, :, t0 - start:t0 - start + width].rearrange("p j (c i) -> p c j i", i=i)
                dst = mixed[:, t0:t0 + width, :].rearrange("p (c i) j -> p c j i", i=i)
                if engine == A:
                    nc.scalar.activation(dst, src, COPY)
                elif engine == V:
                    nc.vector.tensor_copy(dst, src)
                else:
                    nc.gpsimd.tensor_copy(dst, src)
                t0 = t0 + width
                if blocks[0] <= t0 - first:
                    last = first + blocks.pop(0)
                    nc.vector.quantize_mx(
                        out=words[g][:, first:last].bitcast(FP8X4),
                        scales=planes[PLANE_ROW[g]:P, first:last],
                        in_=mixed[:, first:last, :].rearrange("p t j -> p (t j)"),
                    )
                    first = last

        round_and_quantise(0)
        nc.vector.tensor_copy(slot_words[0][:], by_slots(early_words[:, T:], 0, S))

        round_and_quantise(1)
        turned = psum.tile([P, 2, P], F32, name="bank0")
        for r in range(2):
            nc.tensor.transpose(turned[:, r, :], gate_rows[:, r, :], ident[:])
        gate_cols = tile([P, 2 * T // P], F32, "raw1_1152")
        nc.vector.tensor_copy(gate_cols[:].rearrange("p (r c) -> p r c", r=2), turned[:, :, :T // P])
        blocks, fused = T // P, FUSED // P
        copied = [r * blocks + c for r in range(2) for c in range(fused)]
        spreads = [psum.tile([P, 512], F32, name=f"bank{1 + bank}") for bank in range(4)]
        for i, col in enumerate(copied):
            nc.tensor.transpose(spreads[i // 4][:, i % 4 * P:(i % 4 + 1) * P], gate_cols[:, col:col + 1].to_broadcast([P, P]), ident[:])
        pair_gates = []
        for bank, (a, z) in enumerate(zip(BOTH_CUTS, BOTH_CUTS[1:])):
            kept = psum.tile([P, 2, z - a], F32, name=f"bank{6 + bank}")
            for r in range(2):
                for c in range(a // P, z // P):
                    col = r * blocks + c
                    nc.tensor.transpose(kept[:, r, c * P - a:(c + 1) * P - a], gate_cols[:, col:col + 1].to_broadcast([P, P]), ident[:])
            pair_gates.append(kept)
        nc.vector.tensor_copy(slot_words[1][:], by_slots(early_words[:, :2 * (S - HELD)], 0, S - HELD))

        round_and_quantise(2)
        held = tile([P, HELD], U32, "raw2_1024")
        nc.vector.tensor_copy(held[:], by_slots(words[1], S - HELD, S))

        gates = tile([P, 2 * FUSED], F32, "mixed2")
        for bank, spread in enumerate(spreads):
            width = min(512, 2 * FUSED - 512 * bank)
            nc.scalar.copy(gates[:, 512 * bank:512 * bank + width], spread[:, :width])

        for a, z in zip(BYTE_CUTS, BYTE_CUTS[1:]):
            nc.vector.tensor_copy(slot_planes[:, a:z], by_slots(planes[:], a, z))
            for g in (1, 2):
                k = PLANE_ROW[g]
                for r in (32 * q for q in QUADRANTS):
                    nc.sync.dma_start(moved[g][r:r + 4, a:z].bitcast(I32), slot_planes[r + k:r + k + 4, a:z].bitcast(I32))

        for a, z in zip(LAST_CUTS, LAST_CUTS[1:]):
            nc.vector.tensor_copy(slot_words[2][:, a:z], by_slots(last_words[:], a, z))

        def multiply(acc, e, lo, hi, g, opens=True, closes=True):
            s0 = e * C
            codes = held[:, lo:hi] if e == E - 1 and g == 1 else slot_words[g][:, s0 + lo:s0 + hi]
            nc.tensor.matmul_mx(
                out=acc[:, lo:hi],
                lhsT=w_sb[:, e * PASSES + g, :].bitcast(FP4X4),
                lhsT_scale=ws_sb[:, e * PASSES + g, :],
                rhs=codes.bitcast(FP8X4),
                rhs_scale=moved[g][:, s0 + lo:s0 + hi],
                start=(g == 0 and opens),
                stop=(g == PASSES - 1 and closes),
            )

        banks = [psum.tile([P, 2, C], F32, name=f"bank{i}") for i in range(6)]
        place = {0: (banks[0][:, 0, :], True, False), 1: (banks[0][:, 1, :], False, True), 2: (banks[1][:, 0, :], True, True),
                 3: (banks[2][:, 0, :], True, False), 4: (banks[2][:, 1, :], False, True), 5: (banks[3][:, 0, :], True, True),
                 6: (banks[4][:, 0, :], True, True)}

        def product(e, g):
            multiply(place[e][0], e, 0, C, g, place[e][1], place[e][2])

        def gelu(acc, e, lo, hi):
            nc.scalar.activation(y[:, e * C + lo:e * C + hi], acc[:, lo:hi], GELU, bias=bias[:, e:e + 1])

        def close(experts):
            for e in experts:
                product(e, PASSES - 1)
            for e in experts:
                gelu(place[e][0], e, 0, C)

        last = E - 1
        ahead = BYTE_CUTS[1] // C
        for e in range(last):
            product(e, 0)
        multiply(banks[5][:, 0, :], last, 0, P, 0)
        for e in range(ahead):
            product(e, 1)
        close((0, 1))
        close((2,))
        extra = psum.tile([P, 2, C], F32, name="bank0")
        multiply(extra[:, 0, :], last, P, C, 0)
        close((3, 4))
        for e in range(ahead, last):
            product(e, 1)
        halves = ((banks[5][:, 0, :], 0, P), (extra[:, 0, :], P, C))
        for acc, lo, hi in halves:
            multiply(acc, last, lo, hi, 1)
        for e in range(ahead, last):
            close((e,))
        for acc, lo, hi in halves:
            multiply(acc, last, lo, hi, PASSES - 1)
            gelu(acc, last, lo, hi)

        lists = (pos1_sb, pos2_sb)
        gate_of = gates[:].rearrange("p (r t) -> p r t", r=2)

        def looked_up(r, a, z):
            return y[:].indirect(lists[r][:, a // 16:z // 16])

        first = tile([P, FUSED], F32, "first")
        nc.vector.tensor_tensor(first[:], looked_up(0, 0, FUSED), gates[:, :FUSED], MULT)
        sums = []
        for a, z in zip(SECOND_CUTS, SECOND_CUTS[1:]):
            plain = tile([P, z - a], F32, f"plain{a}")
            nc.scalar.activation(plain[:], looked_up(1, a, z), COPY)
            second = tile([P, z - a], F32, f"second{a}")
            nc.vector.tensor_tensor(second[:], plain[:], gate_of[:, 1, a:z], MULT)
            sums.append((first[:, a:z], second[:], a, z))

        def add_and_store(one, other, a, z, engine=nc.vector):
            total = tile([P, z - a], F32, f"total{a}")
            engine.tensor_tensor(total[:], one, other, ADD)
            nc.sync.dma_start(out[:, a:z], total[:])

        add_and_store(*sums[0])
        add_and_store(*sums[1], nc.gpsimd)
        sums = []
        for kept, (a, z) in zip(pair_gates, zip(BOTH_CUTS, BOTH_CUTS[1:])):
            pair = tile([P, 2, z - a], F32, f"pair{a}")
            for r in range(2):
                nc.scalar.activation(pair[:, r, :], looked_up(r, a, z), COPY)
            gated = tile([P, 2, z - a], F32, f"gated{a}")
            nc.vector.tensor_tensor(gated[:], pair[:], kept[:], MULT)
            sums.append((gated[:, 0, :], gated[:, 1, :], a, z))
        for part in sums:
            add_and_store(*part)
